import numpy as np, ml_dtypes
CORES = [40,64,80,88,96,104,120,144]
N = 8
import mx_ref
BF = ml_dtypes.bfloat16
def gcols(t, e):
    v = np.concatenate([t.reshape(8, 16, -1, 4), np.zeros((8, 16, 1, 4), BF)], axis=2)
    return np.ascontiguousarray(np.stack([v[g][:, e[g]] for g in range(8)])).reshape(128, -1)
def gpick(z, e):
    return np.concatenate([z[16 * g:16 * g + 16][:, e[g]] for g in range(8)])
def tile(rs):
    return np.stack(rs, axis=2).reshape(128, -1).astype(BF)
def pick(q, e):
    c = np.concatenate([q[0].reshape(128, -1, 4), np.zeros((128, 1, 4), np.uint8)], axis=1); s = np.concatenate([q[1], np.ones((16, 1), np.uint8)], axis=1)
    return (np.ascontiguousarray(c[:, e].reshape(128, -1)), np.ascontiguousarray(s[:, e]))
def join(*qs):
    return (np.concatenate([q[0] for q in qs], axis=1), np.concatenate([q[1] for q in qs], axis=1))
def put(q, e, v):
    c, s = q[0].reshape(128, -1, 4).copy(), q[1].copy(); c[:, e] = v[0].reshape(128, -1, 4); s[:, e] = v[1]
    return (c.reshape(128, -1), s)
def pk(c, s):
    return (np.ascontiguousarray(c), mx_ref.live(s))
def emit(q):
    return q[0], q[1]
def packed(v, rng):
    q = [mx_ref.quantize(np.ascontiguousarray(v[r])) for r in range(N)]
    return np.stack([a for a, b in q]), np.stack([mx_ref.plane(b, rng) for a, b in q])
def values_of_codes():
    e, c = np.zeros((128, 128, 4), np.float32), np.zeros((128, 2, 4), np.uint8)
    e[np.arange(128), np.arange(128), 0] = 1
    c[:127, :, 0] = np.arange(256).reshape(2, 128).T[:127]
    return mx_ref.matmul(mx_ref.quantize(e.reshape(128, 512).astype(BF)), (c.reshape(128, 8), np.full((16, 2), 127, np.uint8))).T.reshape(-1).astype(np.float64)
CODE_VALUE, SCALE_VALUE = values_of_codes(), 2.0 ** (np.arange(256) - 127.0)
def decode(q):
    return (CODE_VALUE[q[0]].reshape(16, 8, -1, 4) * SCALE_VALUE[q[1]][:, None, :, None] + 0.0).reshape(128, -1).astype(np.float32)
def f(rng, *shape):
    return mx_ref.flush((rng.standard_normal(shape, dtype=np.float32) * np.exp2(rng.integers(-2, 3, shape[:-1] + (1,)))).astype(BF))
def wide(rng, *shape, cols=0):
    v = rng.standard_normal(shape, dtype=np.float32) * np.exp2(rng.integers(-12, 13, shape)).astype(np.float32)
    if cols: v *= np.repeat(np.exp2(rng.integers(-cols, cols + 1, shape[:-2] + (1, shape[-1] // 4))) * (rng.random(shape[:-2] + (1, shape[-1] // 4)) > 0.0625), 4, axis=-1).astype(np.float32)
    return mx_ref.flush(v.astype(BF))
C, H, E, K, J, R = 288, 96, 384, 64, 3, 2
def big(v):
    v = v.astype(np.float32)
    v[np.abs(v) < np.float32(2.0 ** -16)] = 0
    return v.astype(BF)
def numbers_of(rng):
    return {"x": big(f(rng, N, 128, 4 * C)), "u": np.array(f(rng, N, 128, 512)), "v": np.array(f(rng, N, 128, 512))}
def layers(rng):
    return big(f(rng, N, 128, 2048)).reshape(N, 8, 16, 4, 8, 16, 4)
def weights(rng, w):
    c, p = packed(np.ascontiguousarray(w).reshape(N, 128, 2048), rng)
    return {"wc": c, "ws": p}
def setup_inputs(rng):
    return {**numbers_of(rng), **weights(rng, layers(rng))}
def setup_inputs_ties(rng):
    d = numbers_of(rng)
    x = d["x"].reshape(N, 8, 16, C, 4)
    x[:, :, 0] = 0
    x[:, :, 0, :, 0] = rng.integers(0, 3, (N, 8, C)).astype(np.float32).astype(BF)
    u = d["u"].reshape(N, 128, 128, 4)
    u[:, :, ::16] = 0
    o = rng.permutation(N)
    for r in range(N):
        for h in range(0, 128, 16): u[r, h, h, 0] = 0.0 if r == o[0] else -1.0 if r == o[1] else 1.0
    w = layers(rng)
    w[:, :, :, :, :, 0] = 0
    return {"x": x.reshape(N, 128, 4 * C), "u": u.reshape(N, 128, 512), "v": d["v"], **weights(rng, w)}
def setup_inputs_near(rng):
    d = numbers_of(rng)
    x = d["x"].astype(np.float32).reshape(N, 8, 16, C, 4)
    u = d["u"].reshape(N, 128, 128, 4)
    o = rng.permutation(N) % 4
    x[:, :, :2] = 0
    x[:, :, 8:] = 0
    x[:, :, 0, :, 0] = 1
    u[:, :, ::16] = 0
    for r in range(N):
        s = rng.integers(0, 16, (8, C))
        low = rng.permutation(8)[:4]
        if o[r] == 3: s[low] = s[low] % 4
        x[r, :, 8] = ((s[:, :, None] >> np.arange(4)) & 1) * np.exp2(np.arange(4) - (23.0 if o[r] < 2 else 28.0))
        if o[r] == 3: x[r, low, 9] = x[r, low, 8]
        if o[r] < 2: x[r, :, 11, :, 0] = 2.0 ** -10
        for g in rng.permutation(8)[:4]: x[r, g, 1, rng.integers(C), 0] = 2.0 ** 28 * rng.choice([-1.0, 1.0])
        k = (1.0, -2.0 ** -30, 2.0 ** -30, -2.0 ** -30)[o[r]]
        for h in range(0, 128, 16):
            u[r, h + 8, h] = k
            if o[r] < 2:
                u[r, h, h, 0] = k
                u[r, h + 11, h, 0] = k
            if o[r] == 2: u[r, h + 1, h, 0] = 1.0
            if o[r] == 3 and h // 16 in low:
                u[r, h + 8, h] = -k
                u[r, h + 9, h] = 1.125 * k
    w = layers(rng)
    for i in (0, 1, 8, 9, 10, 11, 12, 13, 14, 15):
        w[:, :, i] = 0
        w[:, :, :, :, :, i] = 0
    return {"x": x.reshape(N, 128, 4 * C).astype(BF), "u": u.reshape(N, 128, 512), "v": d["v"], **weights(rng, w)}
def setup_inputs_huge(rng):
    d = numbers_of(rng)
    o = rng.permutation(N)
    c = rng.integers(0, 2, (N, 1, 1, C, 1))
    odd = np.arange(16).reshape(1, 1, 16, 1, 1) % 2
    x = np.where(c == odd, 2.0 ** 30 * (0.7 + 0.05 * rng.random((N, 8, 16, C, 4))), 2.0 ** 28 * (0.9 + 0.1 * rng.random((N, 8, 16, C, 4))))
    x[o == 0] = 2.0 ** 30 * (0.75 + 0.0625 * rng.integers(0, 3, (1, 8, 16, C, 4)))
    a = 2.0 ** 30 * (1.0 - 0.1 * rng.random((N, 8, 16, 8, 4)))
    for r in range(N):
        if o[r] == 0: a[r] = 2.0 ** 30 * (rng.permutation(8) % 2 * 2.0 - 1.0)[None, None, :, None]
        elif o[r] < N // 2: a[r] *= -1.0
        else: a[r] *= (1.0 - 2.0 * odd[0]) * rng.choice([-1.0, 1.0], (1, 1, 8, 1))
    u = d["u"].reshape(N, 128, 128, 4)
    u[:, :, ::16] = a.reshape(N, 128, 8, 4).astype(np.float32).astype(BF)
    w = np.zeros((N, 128, 4, 128, 4), np.float32)
    i = np.arange(128)
    for b in range(4): w[:, i, b, i, b] = -1
    return {"x": x.astype(np.float32).reshape(N, 128, 4 * C).astype(BF), "u": u.reshape(N, 128, 512), "v": d["v"], **weights(rng, w.astype(BF))}
def setup_inputs_long(rng):
    d = numbers_of(rng)
    x = d["x"].astype(np.float32).reshape(N, 8, 16, C, 4)
    x[:, :, 0] = 0
    x[:, :, 0, 1::2, 0] = 1
    s = np.arange(E) % 2
    s[E - 2:] = 1, 0
    m = E // 32
    far = np.concatenate([[m - 1], np.arange(m - 3, 0, -1), [0, m - 2]])
    less = np.concatenate([[m - 1], np.arange(m - 3, 0, -1), [m - 2, 0]])
    t = np.stack([m - 1 - far, m - 1 - less, far[::-1], less[::-1]])[rng.integers(0, 4, (N, 32))].reshape(N, E)
    for r in range(N):
        x[r, :, 0, :, 1 + r % 2] = s[:C]
        x[(r + 1) % N, :, 0, :H, 1 + r % 2] = s[C:]
        x[r, :, 1, :, 1 + r % 2] = t[r, :C]
        x[(r + 1) % N, :, 1, :H, 1 + r % 2] = t[r, C:]
    n = (N, 8, 8, C, 4)
    x[:, :, 8:] = (1.0 + (2 * rng.integers(0, 4, n) + 1) * 0.125) * np.exp2(12.0 - rng.integers(8, 15, n)) * (rng.integers(0, 2, n) * 2.0 - 1.0)
    x[:, :, 8, :, 0] = np.where(rng.random((N, 8, C)) < 0.5, 1.96875, 0.0625) * 2.0 ** 12
    u = d["u"].reshape(N, 128, 128, 4)
    for r in range(N):
        k = rng.permutation(8)
        for g in range(8):
            if k[g] < 7:
                u[r, :, 16 * g] = 0
                u[r, 16 * g + (1 if k[g] == 6 else 0), 16 * g, 0 if k[g] < 5 else 1 + r % 2] = -1.0 if k[g] in (3, 4) else 1.0
    w = layers(rng)
    w[:, :, :9] = 0
    return {"x": x.reshape(N, 128, 4 * C).astype(BF), "u": u.reshape(N, 128, 512), "v": d["v"], **weights(rng, w)}
def setup_inputs_spread(rng):
    d = setup_inputs(rng)
    d["x"] = big(wide(rng, N, 128, 4 * C, cols=6))
    return d
def check_inputs(d):
    b = []
    for k in ("x", "u", "v"):
        a = np.abs(d[k].astype(np.float32))
        if not (np.isfinite(a).all() and ((a == 0) | (a >= 2.0 ** -30) & (a <= 2.0 ** 30)).all()): b.append("a value of " + k)
    none, least, most = [emit(mx_ref.quantize(np.full((128, 16), k, np.float32).astype(BF)))[1][0, 0] for k in (0.0, 2.0 ** -30, 2.0 ** 30)]
    for r in range(N):
        if ((d["wc"][r] == 0x7F) | (d["wc"][r] == 0xFF)).any(): b.append("wc: a code that is no number")
        s = mx_ref.live(d["ws"][r])
        if ((s != none) & ((s < least) | (s > most))).any(): b.append("ws: a scale out of range")
    return b
def reference(x, u, v, wc, ws):
    qu = [mx_ref.quantize(u[r]) for r in range(N)]
    lay = [pk(wc[r], ws[r]) for r in range(N)]
    now = [x[r] for r in range(N)]
    mirror = np.zeros((N, 8, E), np.int64)
    place = np.arange(E)
    for t in range(R):
        q = [mx_ref.quantize(now[r]) for r in range(N)]
        left, away, far = [], [], []
        for r in range(N):
            window = join(q[r], pick(q[(r + 1) % N], np.arange(H)))
            s = mx_ref.matmul(qu[r], window)[::16] + np.float32(0.0)
            full = decode(window).astype(BF)
            standing = np.argsort(np.argsort(-s, axis=1, kind="stable"), axis=1)
            o = np.argsort(place + standing // 32, axis=1, kind="stable")
            end = np.maximum.accumulate(o, axis=1) == place
            b = np.minimum.accumulate(np.where(end, place, E)[:, ::-1], axis=1)[:, ::-1]
            a = np.concatenate([np.zeros((8, 1), np.int64), np.maximum.accumulate(np.where(end, place + 1, 0), axis=1)[:, :-1]], axis=1)
            mirror[r] = np.take_along_axis(o, a + b - place, axis=1)
            z = (gcols(full, o[:, :C]).astype(np.float32) - gcols(full, mirror[r][:, :C]).astype(np.float32) * np.float32(0.5)).astype(BF)
            e = np.argsort(-np.abs(o - place)[:, :C], axis=1, kind="stable")[:, :K]
            left.append(z)
            away.append(e)
            far.append(mx_ref.quantize(gcols(z, e)))
        for r in range(N):
            back = np.full((8, C), K)
            np.put_along_axis(back, away[r], np.arange(K)[None, :], axis=1)
            rows = []
            for b in range(4):
                p = mx_ref.matmul(pick(lay[r], np.arange(128 * b, 128 * b + 128)), far[(r - J) % N]) * np.float32(0.03125)
                p = np.concatenate([p, np.zeros((128, 1), np.float32)], axis=1)
                rows.append(gpick(p, back) + left[r][:, b::4].astype(np.float32))
            now[r] = tile(rows)
    y, lm = np.zeros((N, 128, C), np.float32), np.zeros((N, 8, E), np.float32)
    oc, osc = np.zeros((N, 128, 4 * C), np.uint8), np.zeros((N, 16, C), np.uint8)
    for r in range(N):
        q = mx_ref.quantize(now[r])
        y[r] = mx_ref.matmul(mx_ref.quantize(v[r]), q)
        lm[r] = mirror[r]
        oc[r], osc[r] = emit(q)
    return {"y": y, "lm": lm, "oc": oc, "osc": osc}

@@ -1,0 +1,546 @@
+import numpy as np
+from concourse.mybir import dt, AluOpType, ActivationFunctionType
+
+C, H, E, K, J, R = 288, 96, 384, 64, 3, 2
+X4, U8, U16, BF, F32, I32 = "float8_e4m3fn_x4", "uint8", "uint16", "bfloat16", "float32", "int32"
+
+
+def sb(n, d):
+    return ("sbuf", [128, n], d)
+
+
+SCRATCH = {
+    "ut": sb(512, BF), "vt": sb(512, BF), "uq": sb(128, X4), "us": sb(128, U8), "urq": sb(128, X4), "urs": sb(128, U8),
+    "vq": sb(128, X4), "vs": sb(128, U8), "wq": sb(512, X4), "wp": sb(512, U8),
+    "pi": sb(2, I32), "ci": sb(8, I32), "cf": sb(16, F32), "expi": sb(8, I32), "t16": sb(E, BF), "tt": sb(E, F32), "zs": sb(E, BF),
+    "pku": sb(8, U16), "rgi": sb(4, F32), "rgo": sb(2, U16), "posc": sb(24, F32), "ygf": sb(24, F32), "ygo": sb(24, U16),
+    "maskw": sb(E, BF), "capw": sb(E, BF), "rstw": sb(E, BF), "segr": sb(608, BF), "rst32": sb(768, BF), "c32": sb(E, BF),
+    "cmu": sb(E, F32), "cv": sb(C, F32), "d0k": sb(E, F32), "d0w": sb(24, F32), "ycw": sb(24, F32), "negt": sb(C, F32),
+    "cs": sb(4, F32), "cs2": sb(4, F32), "ones": sb(512, BF), "et": sb(2048, BF), "eq": sb(512, X4), "es": sb(512, U8),
+    "g1": sb(512, BF), "gt": sb(512, BF), "gq": sb(128, X4), "gs": sb(128, U8),
+    "mm": sb(E, F32), "sc": sb(E, F32), "ta": sb(7 * 4 * E, BF), "ca": sb(7 * E, X4), "sa": sb(7 * E, U8),
+    "rs": sb(24, F32), "rs2": sb(24, F32), "jk3": sb(4800, BF), "ext": sb(E, F32), "bz": sb(768, BF), "bh": sb(768, BF), "bt": sb(768, BF),
+    "yb": sb(E, BF), "kr": sb(416, F32), "kw": sb(24, F32), "junk": sb(24 * 36, BF), "sg": sb(24, F32), "p2": sb(24, F32), "pso": sb(24, U16),
+    "cmx": sb(E, BF), "smn": sb(E + 16, BF), "df": sb(E, BF), "fl": sb(E, BF), "bend": sb(E, F32), "cm": sb(E + 16, BF), "mu": sb(E, F32),
+    "muw": sb(E, F32), "muo": sb(24, U16),
+    "orr": sb(E, F32), "mr": sb(E, F32), "ov": sb(C, F32), "mv": sb(C, F32), "ovo": sb(72, U16), "mvo": sb(72, U16),
+    "ft": sb(4 * E, BF), "fo": sb(4 * C, BF), "hm": sb(4 * C, BF),
+    "dd": sb(C, BF), "da": sb(C, BF), "jk2": sb(C, BF), "sv": sb(1, F32), "ii": sb(C, BF), "gg": sb(C, BF), "cc": sb(C, BF), "xp": sb(320, BF),
+    "tr": sb(608, BF), "sgm": sb(608, BF), "rko": sb(32, U16), "er": sb(C, F32), "ev": sb(K, F32), "evo": sb(16, U16),
+    "t1": sb(4 * K, BF), "at": sb(512, BF), "a32": sb(4 * K, BF), "n32": sb(4 * K, BF), "nw": sb(4 * K, BF), "yo": sb(C, F32),
+}
+for _t in range(R + 1):
+    SCRATCH["x%d" % _t] = sb(4 * C, BF)
+    SCRATCH["q%d" % _t] = sb(E, X4)
+    SCRATCH["s%d" % _t] = sb(E, U8)
+for _t in range(R):
+    SCRATCH["aq%d" % _t] = sb(192, X4)
+    SCRATCH["as%d" % _t] = sb(192, U8)
+BANKS = ["d0", "d1", "d2", "d3", "pa", "pb", "na", "pc"]
+for _b in BANKS:
+    SCRATCH[_b] = ("psum", [128, 512], F32)
+
+NPOOL = 130
+SEMAPHORES = ["sent"] + ["h%d" % t for t in range(R)] + ["f%d" % t for t in range(R)] + ["e%d" % i for i in range(NPOOL)]
+
+A = AluOpType
+ACT = ActivationFunctionType
+BIG = 1e28
+
+
+def routes(T, topo):
+    n = len(T.cores)
+    out = []
+    for r in range(n):
+        c = T.cores[r]
+        dsts = [T.cores[(r - 1) % n], T.cores[(r + J) % n]]
+        need = [not topo.may_write(c, d) for d in dsts]
+        if not any(need):
+            out.append((None, [False, False]))
+            continue
+        ok = [k for k in topo.cores_of(c) if k != c and T.rank_of(k) is None and all(topo.may_write(k, d) for d in dsts)]
+        ok.sort(key=lambda k: (topo.die(k) != topo.die(c), k))
+        out.append((ok[:2], [True, need[1]]))
+    return out
+
+
+def pieces(T, t, which):
+    if which == 0:
+        q, s = T["q%d" % t], T["s%d" % t]
+        return [(q[:, 0:H].bitcast(dt.uint8), q[:, C:E].bitcast(dt.uint8)), (s[:, 0:H], s[:, C:E])]
+    q, s = T["aq%d" % t], T["as%d" % t]
+    return [(q[:, K:2 * K].bitcast(dt.uint8), q[:, 0:K].bitcast(dt.uint8)), (s[:, K:2 * K], s[:, 0:K])]
+
+
+def relay_program(g, core, T, topo, r, part, via):
+    n = len(T.cores)
+    src = T.cores[r]
+    sent = 0
+    for t in range(R):
+        for which in range(2):
+            if not via[which]:
+                continue
+            dst = T.cores[(r - 1) % n] if which == 0 else T.cores[(r + J) % n]
+            sem = T.sem["hf"[which] + str(t)]
+            land = pieces(T, t, which)[part][1]
+            g.wait_ge(sem, len(topo.engines(src, core)))
+            rid, pid = topo.addr(dst, core)
+            g.remote_dma(land, land, sem, T.sem.sent, pid, rid, topo.mask(core, dst))
+            sent += len(topo.engines(core, dst))
+    g.wait_ge(T.sem.sent, sent)
+
+
+def rank_program(g, core, T, topo):
+    rt = routes(T, topo)
+    rank = T.rank_of(core)
+    if rank is None:
+        for r in range(len(T.cores)):
+            if rt[r][0] is not None and core in rt[r][0]:
+                relay_program(g, core, T, topo, r, rt[r][0].index(core), rt[r][1])
+        return
+    n = len(T.cores)
+    Q = {"g": g, "v": g.vector, "a": g.scalar, "p": g.tensor, "s": g.sync}
+
+    ops = []
+    hist = {}
+
+    def V(name, a=0, b=None, s=1):
+        return (name, a, b, s)
+
+    def ind(w, o):
+        return ("ind", w, o)
+
+    def ap(v):
+        if not isinstance(v, tuple):
+            return v
+        if v[0] == "ind":
+            return ap(v[1]).indirect(ap(v[2]))
+        if v[3] == 1:
+            return T[v[0]][:, v[1]:v[2]] if v[2] is not None else T[v[0]][:, v[1]:]
+        return T[v[0]][:, v[1]:v[2]:v[3]]
+
+    def flat(vs):
+        out = []
+        for v in vs:
+            if isinstance(v, tuple):
+                out += [v[1], v[2]] if v[0] == "ind" else [v]
+        return out
+
+    def op(q, fn, reads, writes, grp=None, inc=1, fixed=None, acc=False):
+        me = len(ops)
+        deps = set()
+        rd = flat(reads) + [v[2] for v in writes if v[0] == "ind"]
+        wr = [v[1] if v[0] == "ind" else v for v in writes]
+        for isw, vs in ((False, rd), (True, wr)):
+            for v in vs:
+                w = SCRATCH[v[0]][1][1]
+                psum = v[0] in BANKS
+                m = np.zeros(w, bool)
+                if psum:
+                    m[:] = True
+                else:
+                    m[v[1]:v[2]:v[3]] = True
+                h = hist.setdefault(v[0], [])
+                keep = []
+                for (o, ow, oq, om) in h:
+                    hit = bool((om & m).any())
+                    if o != me and hit and (isw or ow or (psum and oq != q)) and not (acc and oq == q and ow and psum):
+                        deps.add(o)
+                    if isw and hit and not acc:
+                        om = om & ~m
+                    if om.any():
+                        keep.append((o, ow, oq, om))
+                keep.append((me, isw, q, m))
+                hist[v[0]] = keep
+        ops.append({"q": q, "fn": fn, "deps": deps, "ev": grp if grp is not None else ("op", me), "inc": inc, "fixed": fixed})
+        return me
+
+    def emit():
+        members = {}
+        for i, o in enumerate(ops):
+            members.setdefault(o["ev"], []).append(i)
+        know = {q: 0 for q in Q}
+        at = []
+        waits = []
+        used = set()
+        for i, o in enumerate(ops):
+            q = o["q"]
+            ws = []
+            if q is not None:
+                for d in sorted(o["deps"], reverse=True):
+                    if know[q] >> d & 1:
+                        continue
+                    ev = ops[d]["ev"]
+                    assert members[ev][-1] < i
+                    ws.append(ev)
+                    used.add(ev)
+                    for m in members[ev]:
+                        know[q] |= at[m] | (1 << m)
+            at.append(know[q] if q is not None else 0)
+            waits.append(ws)
+        free = [[k, 0, 0] for k in range(NPOOL)]
+        where = {}
+        for i, o in enumerate(ops):
+            q, ev = o["q"], o["ev"]
+            if q is None:
+                where[ev] = o["fixed"]
+                continue
+            for w in waits[i]:
+                Q[q].wait_ge(where[w][0], where[w][1])
+            if o["fn"] is None:
+                continue
+            ins = o["fn"]()
+            if ev in used:
+                if ev not in where:
+                    k = [s for s in free if s[2] & ~at[i] == 0][0]
+                    free.remove(k)
+                    free.append(k)
+                    for m in members[ev]:
+                        k[1] += ops[m]["inc"]
+                        k[2] |= 1 << m
+                    where[ev] = (T.sem["e%d" % k[0]], k[1])
+                ins.then_inc(where[ev][0], o["inc"])
+
+    def ts(out, in0, s1, s2, op0, op1=None, grp=None):
+        def fn():
+            if op1 is None:
+                return g.vector.tensor_scalar(ap(out), ap(in0), ap(s1), None, op0)
+            return g.vector.tensor_scalar(ap(out), ap(in0), ap(s1), ap(s2), op0, op1)
+        return op("v", fn, [in0, s1, s2], [out], grp)
+
+    def tt(out, in0, in1, o, grp=None):
+        return op("v", lambda: g.vector.tensor_tensor(ap(out), ap(in0), ap(in1), o), [in0, in1], [out], grp)
+
+    def cp(out, in_, grp=None):
+        return op("v", lambda: g.vector.tensor_copy(ap(out), ap(in_)), [in_], [out], grp)
+
+    def scan(out, d0, d1, init, op0, op1):
+        return op("v", lambda: g.vector.tensor_tensor_scan(ap(out), ap(d0), ap(d1), ap(init), op0, op1), [d0, d1, init], [out])
+
+    def zero(out, grp=None):
+        return op("v", lambda: g.vector.memset(ap(out), 0.0), [], [out], grp)
+
+    def trp(out, in_, grp=None):
+        return op("v", lambda: g.vector.transpose(ap(out), ap(in_)), [in_], [out], grp)
+
+    def quant(q, s, in_):
+        return op("v", lambda: g.vector.quantize_mx(ap(q), ap(s), ap(in_)), [in_], [q, s])
+
+    def act(out, in_, f, bias=None, scale=None, accum=None, grp=None):
+        def fn():
+            kw = {}
+            if bias is not None:
+                kw["bias"] = ap(bias)
+            if scale is not None:
+                kw["scale"] = ap(scale)
+            if accum is not None:
+                kw["accum_out"] = ap(accum)
+            return g.scalar.activation(ap(out), ap(in_), f, **kw)
+        return op("a", fn, [in_, bias, scale], [out] + ([accum] if accum is not None else []), grp)
+
+    def fill(out, m, c, grp=None):
+        return act(out, V("zs", 0, m), ACT.Identity, bias=c, grp=grp)
+
+    def mm(out, w, ws, x, xs, start=True, stop=True, grp=None):
+        return op("p", lambda: g.tensor.matmul_mx(ap(out), ap(w), ap(ws), ap(x), ap(xs), start, stop), [w, ws, x, xs], [out], grp, acc=not start)
+
+    def dma(q, out, in_, reads, writes, grp=None):
+        return op(q, lambda: Q[q].dma_start(out, in_), reads, writes, grp, inc=16)
+
+    def iota(out, pattern, base, cm=0, small=True):
+        def fn():
+            if small:
+                return g.iota(ap(out), pattern, base, cm, allow_small_or_imprecise_dtypes=True)
+            return g.iota(ap(out), pattern, base, cm)
+        return op("g", fn, [], [out])
+
+    def asel(out, in_, pattern, cmp, base, cm, grp=None):
+        return op("g", lambda: g.affine_select(ap(out), ap(in_), pattern, cmp, 0.0, base, cm), [in_], [out], grp)
+
+    sent = [0]
+
+    def send(t, which):
+        dst = T.cores[(rank - 1) % n] if which == 0 else T.cores[(rank + J) % n]
+        src = (rank + 1) % n if which == 0 else (rank - J) % n
+        names = ("q%d" % t, "s%d" % t, 0, H, C, E) if which == 0 else ("aq%d" % t, "as%d" % t, K, 2 * K, 0, K)
+        sem = T.sem["hf"[which] + str(t)]
+        for part in range(2):
+            to = rt[rank][0][part] if rt[rank][1][which] else dst
+            rid, pid = topo.addr(to, core)
+            s_, d_ = pieces(T, t, which)[part]
+            sent[0] += len(topo.engines(core, to))
+            op("g", lambda s_=s_, d_=d_, rid=rid, pid=pid, to=to: g.remote_dma(d_, s_, sem, T.sem.sent, pid, rid, topo.mask(core, to)),
+               [V(names[part], names[2], names[3])], [])
+        total = 0
+        for part in range(2):
+            last = rt[src][0][part] if rt[src][1][which] else T.cores[src]
+            total += len(topo.engines(last, core))
+        op(None, None, [], [V(names[0], names[4], names[5]), V(names[1], names[4], names[5])], fixed=(sem, total))
+
+    RC, R4, B4, PR, GP, PR2, YC, OFW, OFV, NV, RG, R33, YG = [V("cf", i, i + 1) for i in range(13)]
+
+    dma("s", T.x0[:, 0:512], T.x[:, 0:512], [], [V("x0", 0, 512)])
+    dma("a", T.ut[:], T.u[:], [], [V("ut")])
+    dma("s", T.x0[:, 512:4 * C], T.x[:, 512:4 * C], [], [V("x0", 512, 4 * C)])
+
+    def hole(c):
+        zero(V("ta", 4 * (E + 64) * c, 4 * (E + 64) * c + (512 if c == 0 else 256)), "hole")
+
+    iota(V("pi", 0, 1), [[0, 1]], 0, 1, False)
+    iota(V("t16"), [[0, 24], [1, 16]], 0)
+    iota(V("expi"), [[16, 8]], 0, 0, False)
+    iota(V("tt"), [[1, E]], 0)
+    P = V("pi", 0, 1)
+    zero(V("zs"))
+    hole(1)
+    ts(V("ci", 0, 1), P, 15, None, A.bitwise_and, grp="ci")
+    ts(V("ci", 1, 2), P, 2, 3, A.arith_shift_right, A.bitwise_and, grp="ci")
+    ts(V("ci", 2, 3), P, 3, None, A.bitwise_and, grp="ci")
+    ts(V("ci", 4, 5), P, 4, 1, A.arith_shift_right, A.bitwise_and, grp="ci")
+    hole(2)
+    tt(V("ci", 5, 6), V("ci", 0, 1), V("ci", 4, 5), A.add)
+    hole(3)
+    ts(V("ci", 3, 4), V("ci", 5, 6), 1, None, A.bitwise_and)
+    hole(4)
+    cp(V("cf", 0, 5), V("ci", 0, 5))
+    hole(0)
+    ts(V("maskw"), V("t16"), RC, None, A.is_equal)
+    ts(V("cs"), V("t16", 0, 4), R4, 8704.0, A.is_equal, A.mult)
+    cp(V("pku"), V("expi"))
+    hole(5)
+    fill(V("ones", 0, E), E, 1.0, "ones")
+    fill(V("ones", E, 512), 512 - E, 1.0, "ones")
+    for k in range(1, 4):
+        fill(V("ta", 6 * 4 * E + k, 7 * 4 * E, 4), E, 0.0, "zero")
+    act(V("rstw"), V("t16"), ACT.Identity, bias=-BIG, scale=2 * BIG)
+    act(V("capw"), V("maskw"), ACT.Identity, bias=-BIG, scale=2 * BIG)
+
+    def consts_act1():
+        act(OFW, RC, ACT.Identity, bias=7680.0, scale=-512.0, grp="pad0")
+        act(R33, RC, ACT.Identity, bias=6400.0, scale=33.0, grp="pad0")
+        act(YC, RC, ACT.Identity, bias=6160.5 - 7680.0, scale=512.0, grp="pad0")
+        act(YG, GP, ACT.Identity, bias=RC, scale=16.0, grp="pad0")
+        act(PR2, PR, ACT.Identity, bias=15.0, scale=304.0, grp="pad0")
+        act(V("cs2"), V("cs"), ACT.Identity, bias=-512.0, grp="pad0")
+        act(RG, R4, ACT.Identity, bias=B4, scale=-2048.0, grp="pad0")
+        fill(V("rs", 0, 1), 1, 0.0, "pad")
+        act(V("ycw"), V("tt", 0, E, 16), ACT.Identity, bias=YC, scale=-1.0, grp="pad")
+        act(V("ygf"), V("tt", 0, E, 16), ACT.Identity, bias=YG, scale=2.0, grp="pad")
+        act(V("d0w"), V("tt", 0, E, 16), ACT.Identity, bias=R33, scale=33.0, grp="pad")
+        act(NV, RC, ACT.Identity, bias=-0.5, scale=-1.0, grp="pad")
+        act(OFV, RG, ACT.Identity, bias=6144.0, grp="pad")
+
+    def consts_act2():
+        act(V("cmu"), V("maskw"), ACT.Identity, bias=-512.0, scale=33280.0)
+        fill(V("bz", 0, E), E, 0.0, "bz")
+        fill(V("bz", E, 2 * E), E, 0.0, "bz")
+        for s in range(4):
+            act(V("cv", s, C, 4), V("zs", 0, C // 4), ACT.Identity, bias=V("cs2", s, s + 1), grp="cv")
+
+    def consts_g():
+        asel(V("g1"), V("ones"), [[-16, 8], [0, 64]], A.is_ge, 0, 1)
+        asel(V("et", 0, 512), V("ones"), [[-4, 128], [-1, 4]], A.is_equal, 0, 4, "et")
+        asel(V("gt"), V("g1"), [[16, 8], [0, 64]], A.is_ge, 15, -1)
+        for b in range(1, 4):
+            asel(V("et", 512 * b, 512 * b + 512), V("ones"), [[-4, 128], [-1, 4]], A.is_equal, b, 4, "et")
+        iota(V("rst32"), [[0, 24], [8192, 32]], 0)
+        iota(V("d0k"), [[33, E]], 6400)
+        iota(V("kr", 0, 16), [[0, 16]], 0)
+        iota(V("kr", 400, 416), [[0, 16]], -32768)
+        iota(V("c32"), [[0, E]], 32)
+        iota(V("smn", E, E + 16), [[0, 16]], 4096)
+        iota(V("cm", 0, 1), [[0, 1]], 1024)
+        iota(V("posc"), [[32, 24]], 15)
+        iota(V("negt"), [[-1, C]], 0)
+        iota(V("xp", 0, 16), [[0, 16]], 0)
+        iota(V("xp", 304, 320), [[0, 16]], 0)
+        iota(V("segr"), [[0, 38], [4096, 16]], -2048)
+        iota(V("at", 4 * K, 512), [[0, 4 * K]], 0)
+
+    GQ, GS = V("gq"), V("gs")
+
+    def slot(k, lo, hi):
+        return V("ta", 4 * E * (k // 4) + 4 * lo + k % 4, 4 * E * (k // 4) + 4 * hi, 4)
+
+    def sw(k):
+        return V("sc", 16 * k + 15, 16 * k + 16)
+
+    fin = []
+    for t in range(R):
+        X, XN = "x%d" % t, "x%d" % (t + 1)
+        q, s = "q%d" % t, "s%d" % t
+        aq, as_ = "aq%d" % t, "as%d" % t
+        last = t == R - 1
+        quant(V(q, 0, 128), V(s, 0, 128), V(X, 0, 512))
+        send(t, 0)
+        if t == 0:
+            consts_g()
+            dma("s", T.wq[:].bitcast(dt.uint8), T.wc[:], [V(q, 0, 128)], [V("wq")])
+            dma("s", T.wp[:], T.ws[:], [], [V("wp")])
+            dma("s", T.vt[:], T.v[:], [], [V("vt")])
+            quant(V("uq"), V("us"), V("ut"))
+        quant(V(q, 128, C), V(s, 128, C), V(X, 512, 4 * C))
+        if t == 0:
+            op("v", lambda: g.vector.tensor_copy(T.urq[:].bitcast(dt.uint32), T.uq[:].bitcast(dt.uint32).indirect(T.pku[:])), [V("uq"), V("pku")], [V("urq")])
+            act(V("urs"), ind(V("us"), V("pku")), ACT.Copy)
+            consts_act1()
+
+        def scores(lo, hi, b0, b1, between=None):
+            mm(V(b0, 0, hi), V("urq"), V("urs"), V(q, 0, hi), V(s, 0, hi))
+            mm(V(b1, 0, hi), V("urq"), V("urs"), V(q, 0, hi), V(s, 0, hi))
+            tt(V("mm", lo, hi), V(b0, lo, hi), V("capw", lo, hi), A.min)
+            if between is not None:
+                between()
+            scan(V("sc", lo, hi), V("rstw", lo, hi), V("mm", lo, hi), 0.0, A.min, A.max)
+
+        def dv(k, grp=None):
+            ts(slot(k, 0, 16 * k + 16), V("pa" if k < 18 else "pc", 0, 16 * k + 16), sw(k), None, A.is_lt, grp=grp)
+
+        def qa(c, lo, hi):
+            quant(V("ca", E * c + lo, E * c + hi), V("sa", E * c + lo, E * c + hi), V("ta", 4 * (E * c + lo), 4 * (E * c + hi)))
+
+        def row(k):
+            act(V("jk3", 8 * k * (k - 1), 8 * k * (k + 1)), slot(k, 0, 16 * k), ACT.Copy, accum=V("rs", k, k + 1), grp=("row", t))
+
+        def both(ks, grp):
+            for k in ks:
+                act(slot(k, 0, 16 * k + 16), V("pb", 0, 16 * k + 16), ACT.Sign, bias=sw(k), scale=-1.0)
+            for k in ks:
+                act(slot(k, 0, 16 * k), slot(k, 0, 16 * k), ACT.Relu, accum=V("rs", k, k + 1), grp=grp)
+                act(slot(k, 16 * k, 16 * k + 16), slot(k, 16 * k, 16 * k + 16), ACT.Relu, grp=grp)
+
+        scores(0, C, "pa", "pb")
+        both((17, 16), ("both", t))
+        for k in range(15, -1, -1):
+            dv(k, ("v2", t, k // 2) if k > 7 else ("v1", t, k // 4))
+            if k > 7 and k % 2 == 0:
+                row(k + 1)
+                row(k)
+            if k == 14:
+                tt(slot(24, 0, C), V("pa", 0, C), V("sc", 0, C), A.is_equal)
+            if k == 10:
+                qa(3, 0, 256)
+            if k == 6:
+                qa(2, 0, 192)
+            if k == 4:
+                for kk in range(7, 3, -1):
+                    row(kk)
+        qa(6, 0, 256)
+        if t == 0:
+            quant(GQ, GS, V("gt"))
+        scores(C, E, "pc", "pb", lambda: qa(1, 0, 128))
+        qa(0, 0, 128)
+        for kk in range(3, 0, -1):
+            row(kk)
+        both((23,), ("both2", t))
+        for k in (22, 21, 20, 19, 18):
+            dv(k)
+            row(k)
+            if k == 22:
+                tt(slot(24, C, E), V("pc", C, E), V("sc", C, E), A.is_equal)
+            if k == 21:
+                qa(6, 256, E)
+        qa(5, 0, E)
+        qa(4, 0, 320)
+        order = [6, 0, 1, 2, 3, 5, 4]
+        for c in order:
+            w = E if c == 6 else max(128, 64 * c + 64)
+            mm(V("na", 0, w), GQ, GS, V("ca", E * c, E * c + w), V("sa", E * c, E * c + w), c == order[0], c == order[-1], grp=("na", t))
+        if t == 0:
+            consts_act2()
+            quant(V("eq"), V("es"), V("et"))
+        for b in range(4):
+            mm(V("d%d" % b, 0, E), V("eq", 128 * b, 128 * b + 128), V("es", 128 * b, 128 * b + 128), V(q, 0, E), V(s, 0, E))
+        for b in range(2 if t else 0):
+            act(V("ft", b, 4 * E, 4), V("d%d" % b, 0, E), ACT.Copy)
+        tt(V("rs2"), V("ycw"), V("rs"), A.add)
+        scan(V("ext"), V("cmu"), V("na", 0, E), 0.0, A.add, A.min)
+        if t == 0:
+            cp(V("ygo"), V("ygf"))
+            ts(V("rgi", 0, 2), V("tt", 0, 32, 16), RC, 16.0, A.add, A.mult)
+        tt(V("bz", 0, 768, 32), V("rs2"), V("ext", 15, E, 16), A.subtract)
+        if t == 0:
+            ts(V("rgo"), V("rgi", 0, 2), PR2, 607.0, A.add, A.min)
+        scan(V("bh"), V("rst32"), V("bz"), 0.0, A.min, A.max)
+        tt(V("kw"), V("d0w"), V("bz", 0, 768, 32), A.subtract)
+        trp(V("bt"), V("bh"))
+        tt(V("kr", 16, 16 + E), ind(V("bt"), V("ygo")), V("d0k"), A.subtract)
+        act(V("yb"), ind(V("bt"), V("ygo")), ACT.Copy)
+        scan(V("cmx"), V("yb"), V("c32"), 8192.0, A.min, A.add)
+        for k in range(24):
+            act(V("junk", 36 * k, 36 * k + 36), V("kr", 6 + 16 * k, 42 + 16 * k), ACT.Sign, bias=V("kw", k, k + 1),
+                accum=V("sg", k, k + 1), grp=("pos", t))
+        for b in range(2 if t else 0, 4):
+            act(V("ft", b, 4 * E, 4), V("d%d" % b, 0, E), ACT.Copy)
+        scan(V("smn", E - 1, None, -1), V("yb", E - 1, None, -1), V("c32"), 0.0, A.max, A.subtract)
+        scan(V("df"), V("smn", 1, E + 1), V("cmx"), 0.0, A.max, A.subtract)
+        ts(V("fl"), V("df"), 0.0, None, A.is_ge)
+        scan(V("bend", E - 1, None, -1), V("fl", E - 1, None, -1), V("tt", E - 1, None, -1), 0.0, A.mult, A.max)
+        ts(V("cm", 1, C + 1), V("fl", 0, C), -1025.0, 1024.0, A.mult, A.add)
+        scan(V("mu", 0, C), V("cm", 0, C), V("bend", 0, C), 0.0, A.add, A.min)
+        scan(V("muw", 0, C), V("cmu", 0, C), V("mu", 0, C), 0.0, A.add, A.min)
+        tt(V("p2"), V("sg"), V("posc"), A.add)
+        ts(V("muo", 0, C // 16), V("muw", 15, C, 16), OFW, None, A.add)
+        ts(V("pso"), V("p2"), 0.5, None, A.mult)
+        cp(ind(V("orr"), V("pso")), V("tt"))
+        act(V("mr", 0, C), ind(V("orr"), V("muo", 0, C // 16)), ACT.Copy)
+        scan(V("dd"), V("negt"), V("orr", 0, C), 0.0, A.min, A.add)
+        act(V("da"), V("dd"), ACT.Abs)
+        scan(V("ov"), V("cv"), V("orr", 0, C), 0.0, A.add, A.min)
+        act(V("jk2"), V("da"), ACT.Sign, bias=NV, accum=V("sv"))
+        ts(V("ovo"), V("ov", 3, C, 4), 4.0, OFV, A.mult, A.add)
+        ts(V("ii"), V("da"), RC, None, A.is_equal)
+        ts(V("gg"), V("da"), RC, -1024.0, A.not_equal, A.mult)
+        act(V("fo"), ind(V("ft"), V("ovo")), ACT.Copy)
+        scan(V("cc"), V("ii"), V("ii"), V("sv"), A.add, A.add)
+        scan(V("mv"), V("cv"), V("mr", 0, C), 0.0, A.add, A.min)
+        scan(V("xp", 16, 304), V("cc"), V("gg"), -1024.0, A.max, A.add)
+        ts(V("mvo"), V("mv", 3, C, 4), 4.0, OFV, A.mult, A.add)
+        act(V("hm"), ind(V("ft"), V("mvo")), ACT.Identity, scale=-0.5)
+        trp(V("tr", 0, C), V("xp", 16, 304), grp=("tr", t))
+        trp(V("tr", C, 608), V("xp"), grp=("tr", t))
+        scan(V("sgm"), V("segr"), V("tr"), 0.0, A.min, A.max)
+        ts(V("rko"), ind(V("sgm"), V("rgo")), 0.5, 143.0, A.mult, A.add)
+        cp(ind(V("er"), V("rko", 0, 18)), V("tt", 0, C))
+        scan(V("ev"), V("cv", 0, K), V("er", 0, K), 0.0, A.add, A.min)
+        ts(V("evo"), V("ev", 3, K, 4), 4.0, OFV, A.mult, A.add)
+        act(V("t1"), ind(V("hm"), V("evo")), ACT.Copy)
+        tt(V("at", 0, 4 * K), ind(V("fo"), V("evo")), V("t1"), A.add)
+        quant(V(aq, K, 192), V(as_, K, 192), V("at"))
+        send(t, 1)
+        act(V("a32"), V("at", 0, 4 * K), ACT.Identity, scale=32.0)
+        if last:
+            ts(V("cm", C + 1, E + 1), V("fl", C, E), -1025.0, 1024.0, A.mult, A.add)
+            tt(V(XN, 0, 2 * C), V("fo", 0, 2 * C), V("hm", 0, 2 * C), A.add)
+            scan(V("mu", C, E), V("cm", C, E), V("bend", C, E), V("mu", C - 1, C), A.add, A.min)
+            tt(V(XN, 2 * C, 3 * C), V("fo", 2 * C, 3 * C), V("hm", 2 * C, 3 * C), A.add)
+            scan(V("muw", C, E), V("cmu", C, E), V("mu", C, E), 0.0, A.add, A.min)
+            tt(V(XN, 3 * C, 4 * C), V("fo", 3 * C, 4 * C), V("hm", 3 * C, 4 * C), A.add)
+            ts(V("muo", C // 16, E // 16), V("muw", C + 15, E, 16), OFW, None, A.add)
+            act(V("mr", C, E), ind(V("orr"), V("muo", C // 16, E // 16)), ACT.Copy)
+            fin.append(dma("s", T.lm[:], T.mr[0:128:16, :], [V("mr")], []))
+        else:
+            tt(V(XN), V("fo"), V("hm"), A.add)
+            quant(V("vq"), V("vs"), V("vt"))
+        for b in range(4):
+            mm(V("d%d" % b, 0, 128), V("wq", 128 * b, 128 * b + 128), V("wp", 128 * b, 128 * b + 128), V(aq, 0, 128), V(as_, 0, 128))
+        for b in range(4):
+            tt(V("n32", b, 4 * K, 4), V("d%d" % b, 0, K), V("a32", b, 4 * K, 4), A.add, grp=("n32", t))
+        ts(V("nw"), V("n32"), 0.03125, None, A.mult)
+        cp(ind(V(XN), V("evo")), V("nw"))
+
+    q, s = "q%d" % R, "s%d" % R
+    hc = C // 2
+    quant(V(q, 0, hc), V(s, 0, hc), V("x%d" % R, 0, 4 * hc))
+    quant(V(q, hc, C), V(s, hc, C), V("x%d" % R, 4 * hc, 4 * C))
+    mm(V("pa", 0, hc), V("vq"), V("vs"), V(q, 0, hc), V(s, 0, hc))
+    mm(V("pb", 0, hc), V("vq"), V("vs"), V(q, hc, C), V(s, hc, C))
+    act(V("yo", 0, hc), V("pa", 0, hc), ACT.Copy)
+    cp(V("yo", hc, C), V("pb", 0, hc))
+    fin.append(dma("s", T.oc[:], T[q][:, 0:C].bitcast(dt.uint8), [V(q, 0, C)], [], grp="outs"))
+    fin.append(dma("a", T.y[:], T.yo[:], [V("yo")], []))
+    for k in range(4):
+        fin.append(dma("s", T.osc[4 * k:4 * k + 4, :], T[s][32 * k:32 * k + 4, 0:C], [V(s, 0, C)], [], grp="outs"))
+    ops.append({"q": "g", "fn": None, "deps": set(fin), "ev": ("end",), "inc": 0, "fixed": None})
+    emit()
+    g.wait_ge(T.sem.sent, sent[0])

@@ -9,25 +9,36 @@ def sb(n, d):
     return ("sbuf", [128, n], d)
 
 
+TILES = [(24, 17, 16, 15), (14, 13, 8, 7), (12, 11, 10, 9), (6, 5, 4, 3), (23, 22, 21, 20), (19, 18, 2, 1)]
+WIDE = [max(128, 16 * max(c)) for c in TILES]
+BASE = [sum(WIDE[:c]) for c in range(len(TILES))]
+TW = sum(WIDE)
+OWNV = 10
+HALOV = 20
+RRV = 4
+KCUT = 144
+PCUT = (0, 6, 14, 24)
+
 SCRATCH = {
     "ut": sb(512, BF), "vt": sb(512, BF), "uq": sb(128, X4), "us": sb(128, U8), "urq": sb(128, X4), "urs": sb(128, U8),
     "vq": sb(128, X4), "vs": sb(128, U8), "wq": sb(512, X4), "wp": sb(512, U8),
-    "pi": sb(2, I32), "ci": sb(8, I32), "cf": sb(16, F32), "expi": sb(8, I32), "t16": sb(E, BF), "tt": sb(E, F32), "zs": sb(E, BF),
+    "ci": sb(8, I32), "cf": sb(16, F32), "expi": sb(8, I32), "t16": sb(E, BF), "tt": sb(E, F32), "zs": sb(E, BF),
     "pku": sb(8, U16), "rgi": sb(4, F32), "rgo": sb(2, U16), "posc": sb(24, F32), "ygf": sb(24, F32), "ygo": sb(24, U16),
     "maskw": sb(E, BF), "capw": sb(E, BF), "rstw": sb(E, BF), "segr": sb(608, BF), "rst32": sb(768, BF), "c32": sb(E, BF),
-    "cmu": sb(E, F32), "cv": sb(C, F32), "d0k": sb(E, F32), "d0w": sb(24, F32), "ycw": sb(24, F32), "negt": sb(C, F32),
-    "cs": sb(4, F32), "cs2": sb(4, F32), "ones": sb(512, BF), "et": sb(2048, BF), "eq": sb(512, X4), "es": sb(512, U8),
-    "g1": sb(512, BF), "gt": sb(512, BF), "gq": sb(128, X4), "gs": sb(128, U8),
-    "mm": sb(E, F32), "sc": sb(E, F32), "ta": sb(7 * 4 * E, BF), "ca": sb(7 * E, X4), "sa": sb(7 * E, U8),
-    "rs": sb(24, F32), "rs2": sb(24, F32), "jk3": sb(4800, BF), "ext": sb(E, F32), "bz": sb(768, BF), "bh": sb(768, BF), "bt": sb(768, BF),
+    "cmu": sb(E, BF), "cv": sb(C, F32), "d0k": sb(448, F32), "d0w": sb(24, F32), "ycw": sb(24, F32), "negt": sb(C, F32),
+    "cs": sb(8, F32), "ones": sb(512, BF), "et": sb(2048, BF), "eq": sb(512, X4), "es": sb(512, U8),
+    "g1": sb(128, BF), "gt": sb(512, BF), "gq": sb(128, X4), "gs": sb(128, U8), "kc": sb(80, F32),
+    "mm": sb(E, F32), "sc": sb(E, F32), "ta": sb(4 * TW, BF), "ca": sb(TW, X4), "sa": sb(TW, U8),
+    "rd": sb(E, BF), "rdc": sb(24, F32), "jv": sb(21 * 320, BF),
+    "rs": sb(24, F32), "rr": sb(E, F32), "ext": sb(E, BF), "bz": sb(768, BF), "bh": sb(768, BF), "bt": sb(768, BF),
     "yb": sb(E, BF), "kr": sb(416, F32), "kw": sb(24, F32), "junk": sb(24 * 36, BF), "sg": sb(24, F32), "p2": sb(24, F32), "pso": sb(24, U16),
     "cmx": sb(E, BF), "smn": sb(E + 16, BF), "df": sb(E, BF), "fl": sb(E, BF), "bend": sb(E, F32), "cm": sb(E + 16, BF), "mu": sb(E, F32),
     "muw": sb(E, F32), "muo": sb(24, U16),
     "orr": sb(E, F32), "mr": sb(E, F32), "ov": sb(C, F32), "mv": sb(C, F32), "ovo": sb(72, U16), "mvo": sb(72, U16),
     "ft": sb(4 * E, BF), "fo": sb(4 * C, BF), "hm": sb(4 * C, BF),
-    "dd": sb(C, BF), "da": sb(C, BF), "jk2": sb(C, BF), "sv": sb(1, F32), "ii": sb(C, BF), "gg": sb(C, BF), "cc": sb(C, BF), "xp": sb(320, BF),
+    "dd": sb(C, BF), "da": sb(C, BF), "jk2": sb(C, BF), "sv": sb(1, F32), "ii": sb(C, F32), "gg": sb(C + 16, BF), "xp": sb(320, BF),
     "tr": sb(608, BF), "sgm": sb(608, BF), "rko": sb(32, U16), "er": sb(C, F32), "ev": sb(K, F32), "evo": sb(16, U16),
-    "t1": sb(4 * K, BF), "at": sb(512, BF), "a32": sb(4 * K, BF), "n32": sb(4 * K, BF), "nw": sb(4 * K, BF), "yo": sb(C, F32),
+    "t1": sb(4 * K, BF), "t2": sb(4 * K, BF), "at": sb(512, BF), "a32": sb(4 * K, BF), "n32": sb(4 * K, BF), "nw": sb(4 * K, BF), "yo": sb(C, F32),
 }
 for _t in range(R + 1):
     SCRATCH["x%d" % _t] = sb(4 * C, BF)
@@ -36,12 +47,13 @@ for _t in range(R + 1):
 for _t in range(R):
     SCRATCH["aq%d" % _t] = sb(192, X4)
     SCRATCH["as%d" % _t] = sb(192, U8)
-BANKS = ["d0", "d1", "d2", "d3", "pa", "pb", "na", "pc"]
+BANKS = ["d0", "d1", "d2", "pa", "pb", "na", "ph", "pd"]
 for _b in BANKS:
     SCRATCH[_b] = ("psum", [128, 512], F32)
 
-NPOOL = 130
-SEMAPHORES = ["sent"] + ["h%d" % t for t in range(R)] + ["f%d" % t for t in range(R)] + ["e%d" % i for i in range(NPOOL)]
+NDMA = 12
+SEMAPHORES = (["sent"] + ["h%d" % t for t in range(R)] + ["f%d" % t for t in range(R)] + ["e%d" % i for i in range(NDMA)]
+              + ["c" + q for q in "vapg"])
 
 A = AluOpType
 ACT = ActivationFunctionType
@@ -160,46 +172,45 @@ def rank_program(g, core, T, topo):
         for i, o in enumerate(ops):
             members.setdefault(o["ev"], []).append(i)
         know = {q: 0 for q in Q}
+        done = {q: 0 for q in Q}
+        count = {q: 0 for q in Q}
         at = []
-        waits = []
-        used = set()
-        for i, o in enumerate(ops):
-            q = o["q"]
-            ws = []
-            if q is not None:
-                for d in sorted(o["deps"], reverse=True):
-                    if know[q] >> d & 1:
-                        continue
-                    ev = ops[d]["ev"]
-                    assert members[ev][-1] < i
-                    ws.append(ev)
-                    used.add(ev)
-                    for m in members[ev]:
-                        know[q] |= at[m] | (1 << m)
-            at.append(know[q] if q is not None else 0)
-            waits.append(ws)
-        free = [[k, 0, 0] for k in range(NPOOL)]
         where = {}
+        ndma = [0]
         for i, o in enumerate(ops):
             q, ev = o["q"], o["ev"]
             if q is None:
                 where[ev] = o["fixed"]
+                at.append(1 << i)
                 continue
-            for w in waits[i]:
+            for d in sorted(o["deps"], reverse=True):
+                if know[q] >> d & 1:
+                    continue
+                w = ops[d]["ev"] if ops[d]["inc"] != 1 or ops[d]["q"] is None else ("op", d)
                 Q[q].wait_ge(where[w][0], where[w][1])
+                for m in (members[w] if w[0] != "op" else [d]):
+                    assert m < i
+                    know[q] |= at[m]
             if o["fn"] is None:
+                at.append(0)
                 continue
             ins = o["fn"]()
-            if ev in used:
+            if o["inc"] == 1:
+                count[q] += 1
+                done[q] |= know[q] | (1 << i)
+                at.append(done[q])
+                where[("op", i)] = (T.sem["c" + q], count[q])
+                ins.then_inc(T.sem["c" + q], 1)
+            elif o["inc"] == 16:
+                at.append(know[q] | (1 << i))
                 if ev not in where:
-                    k = [s for s in free if s[2] & ~at[i] == 0][0]
-                    free.remove(k)
-                    free.append(k)
-                    for m in members[ev]:
-                        k[1] += ops[m]["inc"]
-                        k[2] |= 1 << m
-                    where[ev] = (T.sem["e%d" % k[0]], k[1])
-                ins.then_inc(where[ev][0], o["inc"])
+                    where[ev] = (T.sem["e%d" % ndma[0]], 16 * len(members[ev]))
+                    ndma[0] += 1
+                ins.then_inc(where[ev][0], 16)
+            else:
+                at.append(know[q])
+        for q in "vapg":
+            g.wait_ge(T.sem["c" + q], count[q])
 
     def ts(out, in0, s1, s2, op0, op1=None, grp=None):
         def fn():
@@ -214,11 +225,11 @@ def rank_program(g, core, T, topo):
     def cp(out, in_, grp=None):
         return op("v", lambda: g.vector.tensor_copy(ap(out), ap(in_)), [in_], [out], grp)
 
-    def scan(out, d0, d1, init, op0, op1):
-        return op("v", lambda: g.vector.tensor_tensor_scan(ap(out), ap(d0), ap(d1), ap(init), op0, op1), [d0, d1, init], [out])
+    def scan(out, d0, d1, init, op0, op1, grp=None):
+        return op("v", lambda: g.vector.tensor_tensor_scan(ap(out), ap(d0), ap(d1), ap(init), op0, op1), [d0, d1, init], [out], grp)
 
-    def zero(out, grp=None):
-        return op("v", lambda: g.vector.memset(ap(out), 0.0), [], [out], grp)
+    def zero(out, grp=None, c=0.0):
+        return op("v", lambda: g.vector.memset(ap(out), c), [], [out], grp)
 
     def trp(out, in_, grp=None):
         return op("v", lambda: g.vector.transpose(ap(out), ap(in_)), [in_], [out], grp)
@@ -270,87 +281,98 @@ def rank_program(g, core, T, topo):
             s_, d_ = pieces(T, t, which)[part]
             sent[0] += len(topo.engines(core, to))
             op("g", lambda s_=s_, d_=d_, rid=rid, pid=pid, to=to: g.remote_dma(d_, s_, sem, T.sem.sent, pid, rid, topo.mask(core, to)),
-               [V(names[part], names[2], names[3])], [])
+               [V(names[part], names[2], names[3])], [], inc=0)
         total = 0
         for part in range(2):
             last = rt[src][0][part] if rt[src][1][which] else T.cores[src]
             total += len(topo.engines(last, core))
         op(None, None, [], [V(names[0], names[4], names[5]), V(names[1], names[4], names[5])], fixed=(sem, total))
 
-    RC, R4, B4, PR, GP, PR2, YC, OFW, OFV, NV, RG, R33, YG = [V("cf", i, i + 1) for i in range(13)]
+    RC, R4, B4, PR, GP, GI, YC, OFW, OFV, NV, RG, R33, YG, PR2, NG = [V("cf", i, i + 1) for i in range(15)]
 
     dma("s", T.x0[:, 0:512], T.x[:, 0:512], [], [V("x0", 0, 512)])
     dma("a", T.ut[:], T.u[:], [], [V("ut")])
     dma("s", T.x0[:, 512:4 * C], T.x[:, 512:4 * C], [], [V("x0", 512, 4 * C)])
 
-    def hole(c):
-        zero(V("ta", 4 * (E + 64) * c, 4 * (E + 64) * c + (512 if c == 0 else 256)), "hole")
+    def slot(k, lo, hi):
+        c = [k in tile for tile in TILES].index(True)
+        e = TILES[c].index(k)
+        return V("ta", 4 * (BASE[c] + lo) + e, 4 * (BASE[c] + hi), 4)
 
-    iota(V("pi", 0, 1), [[0, 1]], 0, 1, False)
+    def hole(c):
+        zero(V("ta", 4 * (BASE[c] + 16 * min(TILES[c])), 4 * (BASE[c] + WIDE[c])), "hole")
+
+    P = V("ci", 7, 8)
+    iota(P, [[0, 1]], 0, 1, False)
     iota(V("t16"), [[0, 24], [1, 16]], 0)
     iota(V("expi"), [[16, 8]], 0, 0, False)
-    iota(V("tt"), [[1, E]], 0)
-    P = V("pi", 0, 1)
+    iota(V("kc", 0, 24), [[16, 24]], 0)
+    iota(V("kc", 24, 52), [[-32, 7], [-16, 4]], 17)
+    iota(V("g1"), [[1, 8], [0, 16]], 0)
     zero(V("zs"))
     hole(1)
     ts(V("ci", 0, 1), P, 15, None, A.bitwise_and, grp="ci")
     ts(V("ci", 1, 2), P, 2, 3, A.arith_shift_right, A.bitwise_and, grp="ci")
     ts(V("ci", 2, 3), P, 3, None, A.bitwise_and, grp="ci")
     ts(V("ci", 4, 5), P, 4, 1, A.arith_shift_right, A.bitwise_and, grp="ci")
+    ts(V("ci", 5, 6), P, 4, None, A.arith_shift_right, grp="ci")
     hole(2)
-    tt(V("ci", 5, 6), V("ci", 0, 1), V("ci", 4, 5), A.add)
+    tt(V("ci", 6, 7), V("ci", 0, 1), V("ci", 4, 5), A.add)
     hole(3)
-    ts(V("ci", 3, 4), V("ci", 5, 6), 1, None, A.bitwise_and)
+    ts(V("ci", 3, 4), V("ci", 6, 7), 1, None, A.bitwise_and)
     hole(4)
-    cp(V("cf", 0, 5), V("ci", 0, 5))
+    cp(V("cf", 0, 6), V("ci", 0, 6))
     hole(0)
     ts(V("maskw"), V("t16"), RC, None, A.is_equal)
-    ts(V("cs"), V("t16", 0, 4), R4, 8704.0, A.is_equal, A.mult)
+    ts(V("cs", 0, 4), V("t16", 0, 4), R4, 8704.0, A.is_equal, A.mult)
     cp(V("pku"), V("expi"))
-    hole(5)
     fill(V("ones", 0, E), E, 1.0, "ones")
     fill(V("ones", E, 512), 512 - E, 1.0, "ones")
-    for k in range(1, 4):
-        fill(V("ta", 6 * 4 * E + k, 7 * 4 * E, 4), E, 0.0, "zero")
     act(V("rstw"), V("t16"), ACT.Identity, bias=-BIG, scale=2 * BIG)
+    act(OFW, RC, ACT.Identity, bias=7680.0, scale=-512.0, grp="pad0")
+    act(R33, RC, ACT.Identity, bias=6400.0 - 7680.0, scale=545.0, grp="pad0")
+    act(YG, GP, ACT.Identity, bias=RC, scale=16.0, grp="pad0")
+    act(PR2, PR, ACT.Identity, bias=15.0, scale=304.0, grp="pad0")
+    act(RG, R4, ACT.Identity, bias=B4, scale=-2048.0, grp="pad0")
+    fill(V("rs", 0, 1), 1, 0.0, "pad")
+    act(V("ycw"), V("kc", 26, 50), ACT.Identity, bias=RC, grp="pad")
+    act(V("cs", 4, 8), V("cs", 0, 4), ACT.Identity, bias=-512.0, grp="pad")
+    act(V("ygf"), V("kc", 0, 24), ACT.Identity, bias=YG, scale=2.0, grp="pad2")
     act(V("capw"), V("maskw"), ACT.Identity, bias=-BIG, scale=2 * BIG)
 
-    def consts_act1():
-        act(OFW, RC, ACT.Identity, bias=7680.0, scale=-512.0, grp="pad0")
-        act(R33, RC, ACT.Identity, bias=6400.0, scale=33.0, grp="pad0")
-        act(YC, RC, ACT.Identity, bias=6160.5 - 7680.0, scale=512.0, grp="pad0")
-        act(YG, GP, ACT.Identity, bias=RC, scale=16.0, grp="pad0")
-        act(PR2, PR, ACT.Identity, bias=15.0, scale=304.0, grp="pad0")
-        act(V("cs2"), V("cs"), ACT.Identity, bias=-512.0, grp="pad0")
-        act(RG, R4, ACT.Identity, bias=B4, scale=-2048.0, grp="pad0")
-        fill(V("rs", 0, 1), 1, 0.0, "pad")
-        act(V("ycw"), V("tt", 0, E, 16), ACT.Identity, bias=YC, scale=-1.0, grp="pad")
-        act(V("ygf"), V("tt", 0, E, 16), ACT.Identity, bias=YG, scale=2.0, grp="pad")
-        act(V("d0w"), V("tt", 0, E, 16), ACT.Identity, bias=R33, scale=33.0, grp="pad")
-        act(NV, RC, ACT.Identity, bias=-0.5, scale=-1.0, grp="pad")
-        act(OFV, RG, ACT.Identity, bias=6144.0, grp="pad")
+    def consts_v1():
+        cp(V("ygo"), V("ygf"))
+        ts(V("rgi", 0, 2), V("kc", 0, 2), RC, 16.0, A.add, A.mult)
+        for k in TILES[5][1:]:
+            zero(slot(k, 16 * k, WIDE[5]), "zero")
+        ts(V("rgo"), V("rgi", 0, 2), PR2, 607.0, A.add, A.min)
+        zero(V("bz"), c=-1024.0)
+        zero(V("c32"), c=32.0)
 
     def consts_act2():
         act(V("cmu"), V("maskw"), ACT.Identity, bias=-512.0, scale=33280.0)
-        fill(V("bz", 0, E), E, 0.0, "bz")
-        fill(V("bz", E, 2 * E), E, 0.0, "bz")
+        fill(V("c32", 32, E, 64), 6, 64.0)
+        act(V("d0w"), V("kc", 54, 78), ACT.Identity, bias=R33, grp="pad2")
+        act(NV, RC, ACT.Identity, bias=-0.5, scale=-1.0, grp="pad2")
+        act(OFV, RG, ACT.Identity, bias=6144.0, grp="pad2")
+        fill(V("gg", 0, 1), 1, 1024.0)
+
+    def consts_act3():
         for s in range(4):
-            act(V("cv", s, C, 4), V("zs", 0, C // 4), ACT.Identity, bias=V("cs2", s, s + 1), grp="cv")
+            act(V("cv", s, C, 4), V("zs", 0, C // 4), ACT.Identity, bias=V("cs", 4 + s, 5 + s), grp="cv")
 
     def consts_g():
-        asel(V("g1"), V("ones"), [[-16, 8], [0, 64]], A.is_ge, 0, 1)
-        asel(V("et", 0, 512), V("ones"), [[-4, 128], [-1, 4]], A.is_equal, 0, 4, "et")
-        asel(V("gt"), V("g1"), [[16, 8], [0, 64]], A.is_ge, 15, -1)
-        for b in range(1, 4):
-            asel(V("et", 512 * b, 512 * b + 512), V("ones"), [[-4, 128], [-1, 4]], A.is_equal, b, 4, "et")
-        iota(V("rst32"), [[0, 24], [8192, 32]], 0)
-        iota(V("d0k"), [[33, E]], 6400)
+        iota(V("rst32"), [[0, 24], [8192, 32]], -1024)
+        iota(V("kc", 52, 80), [[2144, 7], [528, 4]], -1056)
+        iota(V("d0k"), [[-2144, 7], [-33, 64]], 1056 - 6400)
+        iota(V("tt"), [[1, E]], 0)
         iota(V("kr", 0, 16), [[0, 16]], 0)
         iota(V("kr", 400, 416), [[0, 16]], -32768)
-        iota(V("c32"), [[0, E]], 32)
         iota(V("smn", E, E + 16), [[0, 16]], 4096)
-        iota(V("cm", 0, 1), [[0, 1]], 1024)
         iota(V("posc"), [[32, 24]], 15)
+        iota(V("cm", 0, 1), [[0, 1]], 1024)
+        for b in range(4):
+            asel(V("et", 512 * b, 512 * b + 512), V("ones"), [[-4, 128], [-1, 4]], A.is_equal, b, 4)
         iota(V("negt"), [[-1, C]], 0)
         iota(V("xp", 0, 16), [[0, 16]], 0)
         iota(V("xp", 304, 320), [[0, 16]], 0)
@@ -358,9 +380,7 @@ def rank_program(g, core, T, topo):
         iota(V("at", 4 * K, 512), [[0, 4 * K]], 0)
 
     GQ, GS = V("gq"), V("gs")
-
-    def slot(k, lo, hi):
-        return V("ta", 4 * E * (k // 4) + 4 * lo + k % 4, 4 * E * (k // 4) + 4 * hi, 4)
+    FB = ["d0", "d1", "d2", "pb"]
 
     def sw(k):
         return V("sc", 16 * k + 15, 16 * k + 16)
@@ -375,7 +395,7 @@ def rank_program(g, core, T, topo):
         send(t, 0)
         if t == 0:
             consts_g()
-            dma("s", T.wq[:].bitcast(dt.uint8), T.wc[:], [V(q, 0, 128)], [V("wq")])
+            dma("s", T.wq[:].bitcast(dt.uint8), T.wc[:], [V(q, C, E)], [V("wq")])
             dma("s", T.wp[:], T.ws[:], [], [V("wp")])
             dma("s", T.vt[:], T.v[:], [], [V("vt")])
             quant(V("uq"), V("us"), V("ut"))
@@ -383,149 +403,226 @@ def rank_program(g, core, T, topo):
         if t == 0:
             op("v", lambda: g.vector.tensor_copy(T.urq[:].bitcast(dt.uint32), T.uq[:].bitcast(dt.uint32).indirect(T.pku[:])), [V("uq"), V("pku")], [V("urq")])
             act(V("urs"), ind(V("us"), V("pku")), ACT.Copy)
-            consts_act1()
+            for e in range(4):
+                ts(V("gt", e, 512, 4), V("g1"), GI, None, A.is_equal, grp="gt")
 
-        def scores(lo, hi, b0, b1, between=None):
-            mm(V(b0, 0, hi), V("urq"), V("urs"), V(q, 0, hi), V(s, 0, hi))
-            mm(V(b1, 0, hi), V("urq"), V("urs"), V(q, 0, hi), V(s, 0, hi))
-            tt(V("mm", lo, hi), V(b0, lo, hi), V("capw", lo, hi), A.min)
-            if between is not None:
-                between()
+        def score(bank, lo, hi):
+            mm(V(bank, 0, hi - lo), V("urq"), V("urs"), V(q, lo, hi), V(s, lo, hi))
+
+        def hold(lo, hi):
             scan(V("sc", lo, hi), V("rstw", lo, hi), V("mm", lo, hi), 0.0, A.min, A.max)
 
-        def dv(k, grp=None):
-            ts(slot(k, 0, 16 * k + 16), V("pa" if k < 18 else "pc", 0, 16 * k + 16), sw(k), None, A.is_lt, grp=grp)
+        def cmp_v(k, grp=None):
+            ts(slot(k, 0, min(C, 16 * k)), V("pa", 0, min(C, 16 * k)), sw(k), None, A.is_lt, grp=grp)
+
+        def count_v(k, grp=None):
+            scan(V("jv", 320 * k + 320 - 16 * k, 320 * k + 320), slot(k, 0, 16 * k), V("zs", 0, 16 * k), -128.0, A.add, A.add, grp=grp)
+
+        def runs(lo, hi):
+            scan(V("rd", lo, hi), V("t16", lo, hi), slot(24, lo, hi), 0.0, A.min, A.add)
 
         def qa(c, lo, hi):
-            quant(V("ca", E * c + lo, E * c + hi), V("sa", E * c + lo, E * c + hi), V("ta", 4 * (E * c + lo), 4 * (E * c + hi)))
+            quant(V("ca", BASE[c] + lo, BASE[c] + hi), V("sa", BASE[c] + lo, BASE[c] + hi), V("ta", 4 * (BASE[c] + lo), 4 * (BASE[c] + hi)))
 
-        def row(k):
-            act(V("jk3", 8 * k * (k - 1), 8 * k * (k + 1)), slot(k, 0, 16 * k), ACT.Copy, accum=V("rs", k, k + 1), grp=("row", t))
-
-        def both(ks, grp):
+        def both(ks, bank, grp):
             for k in ks:
-                act(slot(k, 0, 16 * k + 16), V("pb", 0, 16 * k + 16), ACT.Sign, bias=sw(k), scale=-1.0)
+                act(slot(k, 0, 16 * k), V(bank, 0, 16 * k), ACT.Sign, bias=sw(k), scale=-1.0)
             for k in ks:
                 act(slot(k, 0, 16 * k), slot(k, 0, 16 * k), ACT.Relu, accum=V("rs", k, k + 1), grp=grp)
-                act(slot(k, 16 * k, 16 * k + 16), slot(k, 16 * k, 16 * k + 16), ACT.Relu, grp=grp)
 
-        scores(0, C, "pa", "pb")
-        both((17, 16), ("both", t))
-        for k in range(15, -1, -1):
-            dv(k, ("v2", t, k // 2) if k > 7 else ("v1", t, k // 4))
-            if k > 7 and k % 2 == 0:
-                row(k + 1)
-                row(k)
-            if k == 14:
-                tt(slot(24, 0, C), V("pa", 0, C), V("sc", 0, C), A.is_equal)
-            if k == 10:
-                qa(3, 0, 256)
-            if k == 6:
-                qa(2, 0, 192)
-            if k == 4:
-                for kk in range(7, 3, -1):
-                    row(kk)
-        qa(6, 0, 256)
+        def na(c, first=False, end=False):
+            w = WIDE[c]
+            mm(V("na", 0, w), GQ, GS, V("ca", BASE[c], BASE[c] + w), V("sa", BASE[c], BASE[c] + w), first, end, grp=("na", t))
+
+        def unpack(b):
+            mm(V(FB[b], 0, E), V("eq", 128 * b, 128 * b + 128), V("es", 128 * b, 128 * b + 128), V(q, 0, E), V(s, 0, E))
+            act(V("ft", b, 4 * E, 4), V(FB[b], 0, E), ACT.Copy)
+
+        def pack_e(b):
+            quant(V("eq", 128 * b, 128 * b + 128), V("es", 128 * b, 128 * b + 128), V("et", 512 * b, 512 * b + 512))
+
+        score("pa", 0, C)
+        score("pb", 0, C)
+        cut = 208
+        tt(V("mm", cut, C), V("pa", cut, C), V("capw", cut, C), A.min)
+        tt(V("mm", 0, cut), V("pa", 0, cut), V("capw", 0, cut), A.min)
+        hold(cut, C)
+        hold(0, cut)
+        both((17, 16, 15), "pb", ("both", t, 0))
+        both((14, 13, 12, 11), "pb", ("both", t, 1))
+        for k in range(OWNV, OWNV - 3, -1):
+            cmp_v(k)
+        tt(slot(24, 0, C), V("pa", 0, C), V("sc", 0, C), A.is_le)
+        for k in range(OWNV - 3, 0, -1):
+            cmp_v(k)
+        runs(0, C)
+        for k in range(OWNV, 0, -1):
+            count_v(k)
+        tt(V("rdc", 0, 18), V("rd", 15, C, 16), V("ycw", 0, 18), A.add)
+        qa(3, 0, WIDE[3])
+        ts(V("rs", 1, OWNV + 1), V("jv", 639, 320 * (OWNV + 1), 320), 128.0, None, A.add)
+
+        def counts(step, lo, hi):
+            if step == 0:
+                tt(V("bz", 32 * lo, 32 * hi, 32), V("rdc", lo, hi), V("rs", lo, hi), A.add)
+            elif step == 1:
+                scan(V("bh", 32 * lo, 32 * hi), V("rst32", 32 * lo, 32 * hi), V("bz", 32 * lo, 32 * hi), 0.0, A.min, A.max)
+            elif step == 2:
+                trp(V("bt", 32 * lo, 32 * hi), V("bh", 32 * lo, 32 * hi))
+            elif step == 3:
+                ts(V("rr", 16 * lo, 16 * hi), ind(V("bt", 0, 32 * hi), V("ygo", lo, hi)), 6159.5, None, A.add)
+            else:
+                act(V("rr", 16 * lo, 16 * hi), ind(V("bt", 0, 32 * hi), V("ygo", lo, hi)), ACT.Identity, bias=6159.5)
+
         if t == 0:
+            consts_v1()
             quant(GQ, GS, V("gt"))
-        scores(C, E, "pc", "pb", lambda: qa(1, 0, 128))
-        qa(0, 0, 128)
-        for kk in range(3, 0, -1):
-            row(kk)
-        both((23,), ("both2", t))
-        for k in (22, 21, 20, 19, 18):
-            dv(k)
-            row(k)
-            if k == 22:
-                tt(slot(24, C, E), V("pc", C, E), V("sc", C, E), A.is_equal)
-            if k == 21:
-                qa(6, 256, E)
-        qa(5, 0, E)
-        qa(4, 0, 320)
-        order = [6, 0, 1, 2, 3, 5, 4]
-        for c in order:
-            w = E if c == 6 else max(128, 64 * c + 64)
-            mm(V("na", 0, w), GQ, GS, V("ca", E * c, E * c + w), V("sa", E * c, E * c + w), c == order[0], c == order[-1], grp=("na", t))
+            qa(0, 0, 256)
+            counts(0, 0, 18)
+            qa(1, 0, WIDE[1])
+            counts(1, 0, 18)
+            qa(2, 0, WIDE[2])
+            counts(2, 0, 18)
+            counts(4, 0, 18)
+        score("ph", 256, E)
+        score("pd", 0, E)
+        tt(V("mm", C, E), V("ph", C - 256, 128), V("capw", C, E), A.min)
+        if t > 0:
+            qa(0, 0, 256)
+        hold(C, E)
+        if t > 0:
+            counts(0, 0, 18)
+            qa(1, 0, WIDE[1])
+            counts(1, 0, 18)
+        both(range(23, HALOV, -1), "pd", ("both", t, 2))
+        for k in range(HALOV, 18, -1):
+            ts(slot(k, C, 16 * k), V("ph", C - 256, 16 * k - 256), sw(k), None, A.is_lt)
+        tt(slot(24, C, E), V("ph", C - 256, 128), V("sc", C, E), A.is_le)
+        if t > 0:
+            counts(2, 0, 18)
+        cmp_v(19)
+        runs(C, E)
+        cmp_v(18)
+        qa(0, 256, E)
+        if HALOV > 19:
+            cmp_v(20)
+        tt(V("rdc", 18, 24), V("rd", C + 15, E, 16), V("ycw", 18, 24), A.add)
+        for k in range(18, HALOV + 1):
+            count_v(k)
+        if t > 0:
+            qa(2, 0, WIDE[2])
+            counts(RRV, 0, 18)
+        ts(V("rs", 18, HALOV + 1), V("jv", 320 * 18 + 319, 320 * (HALOV + 1), 320), 128.0, None, A.add)
+        qa(5, 0, WIDE[5])
+        counts(0, 18, 24)
+        qa(4, 0, 192)
+        counts(1, 18, 24)
+        qa(4, 192, WIDE[4])
+        counts(2, 18, 24)
+        if t == 0:
+            pack_e(0)
+        counts(3, 18, 24)
+
+        for c in (0, 1, 3, 2, 5, 4):
+            na(c, c == 0, c == 4)
         if t == 0:
             consts_act2()
-            quant(V("eq"), V("es"), V("et"))
-        for b in range(4):
-            mm(V("d%d" % b, 0, E), V("eq", 128 * b, 128 * b + 128), V("es", 128 * b, 128 * b + 128), V(q, 0, E), V(s, 0, E))
-        for b in range(2 if t else 0):
-            act(V("ft", b, 4 * E, 4), V("d%d" % b, 0, E), ACT.Copy)
-        tt(V("rs2"), V("ycw"), V("rs"), A.add)
-        scan(V("ext"), V("cmu"), V("na", 0, E), 0.0, A.add, A.min)
+        else:
+            for b in range(3):
+                unpack(b)
+        tt(V("yb"), V("rr"), V("na", 0, E), A.subtract)
         if t == 0:
-            cp(V("ygo"), V("ygf"))
-            ts(V("rgi", 0, 2), V("tt", 0, 32, 16), RC, 16.0, A.add, A.mult)
-        tt(V("bz", 0, 768, 32), V("rs2"), V("ext", 15, E, 16), A.subtract)
-        if t == 0:
-            ts(V("rgo"), V("rgi", 0, 2), PR2, 607.0, A.add, A.min)
-        scan(V("bh"), V("rst32"), V("bz"), 0.0, A.min, A.max)
-        tt(V("kw"), V("d0w"), V("bz", 0, 768, 32), A.subtract)
-        trp(V("bt"), V("bh"))
-        tt(V("kr", 16, 16 + E), ind(V("bt"), V("ygo")), V("d0k"), A.subtract)
-        act(V("yb"), ind(V("bt"), V("ygo")), ACT.Copy)
-        scan(V("cmx"), V("yb"), V("c32"), 8192.0, A.min, A.add)
+            pack_e(1)
+        scan(V("ext"), V("cmu"), V("yb"), 0.0, A.add, A.min)
+        scan(V("kr", 16, 16 + KCUT), V("d0k", 32, 32 + KCUT), V("yb", 0, KCUT), 0.0, A.min, A.add)
+        scan(V("cmx"), V("c32"), V("yb"), 8192.0, A.add, A.min)
+        tt(V("kw"), V("d0w"), V("ext", 15, E, 16), A.subtract)
+        scan(V("kr", 16 + KCUT, 16 + E), V("d0k", 32 + KCUT, 32 + E), V("yb", KCUT, E), 0.0, A.min, A.add)
         for k in range(24):
-            act(V("junk", 36 * k, 36 * k + 36), V("kr", 6 + 16 * k, 42 + 16 * k), ACT.Sign, bias=V("kw", k, k + 1),
-                accum=V("sg", k, k + 1), grp=("pos", t))
-        for b in range(2 if t else 0, 4):
-            act(V("ft", b, 4 * E, 4), V("d%d" % b, 0, E), ACT.Copy)
-        scan(V("smn", E - 1, None, -1), V("yb", E - 1, None, -1), V("c32"), 0.0, A.max, A.subtract)
+            act(V("junk", 36 * k, 36 * k + 36), V("kr", 6 + 16 * k, 42 + 16 * k), ACT.Sign, bias=V("kw", k, k + 1), accum=V("sg", k, k + 1))
+        if t == 0:
+            consts_act3()
+        else:
+            unpack(3)
+
+        def position(step, h):
+            lo, hi = PCUT[h], PCUT[h + 1]
+            if step == 0:
+                tt(V("p2", lo, hi), V("sg", lo, hi), V("posc", lo, hi), A.add)
+            elif step == 1:
+                ts(V("pso", lo, hi), V("p2", lo, hi), 0.5, None, A.mult)
+            else:
+                cp(ind(V("orr"), V("pso", lo, hi)), V("tt", 16 * lo, 16 * hi))
+
+        scan(V("smn", E - 1, None, -1), V("yb", E - 1, None, -1), V("c32", E - 1, None, -1), 0.0, A.max, A.subtract)
+        if t == 0:
+            pack_e(2)
         scan(V("df"), V("smn", 1, E + 1), V("cmx"), 0.0, A.max, A.subtract)
-        ts(V("fl"), V("df"), 0.0, None, A.is_ge)
-        scan(V("bend", E - 1, None, -1), V("fl", E - 1, None, -1), V("tt", E - 1, None, -1), 0.0, A.mult, A.max)
+        if t == 0:
+            pack_e(3)
+            for b in range(4):
+                unpack(b)
+        position(0, 0)
+        ts(V("fl"), V("df"), 0.0, None, A.is_gt)
+        position(1, 0)
         ts(V("cm", 1, C + 1), V("fl", 0, C), -1025.0, 1024.0, A.mult, A.add)
+        position(2, 0)
+        position(0, 1)
+        scan(V("bend", E - 1, None, -1), V("fl", E - 1, None, -1), V("tt", E - 1, None, -1), 0.0, A.mult, A.max)
+        position(1, 1)
+        position(0, 2)
         scan(V("mu", 0, C), V("cm", 0, C), V("bend", 0, C), 0.0, A.add, A.min)
+        position(2, 1)
+        position(1, 2)
         scan(V("muw", 0, C), V("cmu", 0, C), V("mu", 0, C), 0.0, A.add, A.min)
-        tt(V("p2"), V("sg"), V("posc"), A.add)
+        position(2, 2)
         ts(V("muo", 0, C // 16), V("muw", 15, C, 16), OFW, None, A.add)
-        ts(V("pso"), V("p2"), 0.5, None, A.mult)
-        cp(ind(V("orr"), V("pso")), V("tt"))
-        act(V("mr", 0, C), ind(V("orr"), V("muo", 0, C // 16)), ACT.Copy)
         scan(V("dd"), V("negt"), V("orr", 0, C), 0.0, A.min, A.add)
-        act(V("da"), V("dd"), ACT.Abs)
         scan(V("ov"), V("cv"), V("orr", 0, C), 0.0, A.add, A.min)
+        act(V("mr", 0, C), ind(V("orr"), V("muo", 0, C // 16)), ACT.Copy)
+        act(V("da"), V("dd"), ACT.Abs)
         act(V("jk2"), V("da"), ACT.Sign, bias=NV, accum=V("sv"))
         ts(V("ovo"), V("ov", 3, C, 4), 4.0, OFV, A.mult, A.add)
-        ts(V("ii"), V("da"), RC, None, A.is_equal)
-        ts(V("gg"), V("da"), RC, -1024.0, A.not_equal, A.mult)
-        act(V("fo"), ind(V("ft"), V("ovo")), ACT.Copy)
-        scan(V("cc"), V("ii"), V("ii"), V("sv"), A.add, A.add)
         scan(V("mv"), V("cv"), V("mr", 0, C), 0.0, A.add, A.min)
-        scan(V("xp", 16, 304), V("cc"), V("gg"), -1024.0, A.max, A.add)
+        act(V("fo"), ind(V("ft"), V("ovo")), ACT.Copy)
+        ts(V("gg", 1, C + 1), V("da"), RC, 1024.0, A.is_equal, A.mult)
         ts(V("mvo"), V("mv", 3, C, 4), 4.0, OFV, A.mult, A.add)
+        ts(V("ii"), V("da"), RC, 1026.0, A.is_equal, A.mult)
         act(V("hm"), ind(V("ft"), V("mvo")), ACT.Identity, scale=-0.5)
-        trp(V("tr", 0, C), V("xp", 16, 304), grp=("tr", t))
-        trp(V("tr", C, 608), V("xp"), grp=("tr", t))
-        scan(V("sgm"), V("segr"), V("tr"), 0.0, A.min, A.max)
+        scan(V("xp", 16, 304), V("ii"), V("gg", 0, C), V("sv"), A.add, A.subtract)
+        trp(V("tr", 0, C), V("xp", 16, 304))
+        trp(V("tr", C, 608), V("xp"))
+        scan(V("sgm", 0, C), V("segr", 0, C), V("tr", 0, C), 0.0, A.min, A.max)
+        scan(V("sgm", C, 608), V("segr", C, 608), V("tr", C, 608), 0.0, A.min, A.max)
         ts(V("rko"), ind(V("sgm"), V("rgo")), 0.5, 143.0, A.mult, A.add)
         cp(ind(V("er"), V("rko", 0, 18)), V("tt", 0, C))
         scan(V("ev"), V("cv", 0, K), V("er", 0, K), 0.0, A.add, A.min)
         ts(V("evo"), V("ev", 3, K, 4), 4.0, OFV, A.mult, A.add)
-        act(V("t1"), ind(V("hm"), V("evo")), ACT.Copy)
-        tt(V("at", 0, 4 * K), ind(V("fo"), V("evo")), V("t1"), A.add)
+        cp(V("t2"), ind(V("fo"), V("evo")))
+        for h in range(2):
+            act(V("t1", 128 * h, 128 * h + 128), ind(V("hm"), V("evo", 8 * h, 8 * h + 8)), ACT.Copy)
+            tt(V("at", 128 * h, 128 * h + 128), V("t1", 128 * h, 128 * h + 128), V("t2", 128 * h, 128 * h + 128), A.add)
         quant(V(aq, K, 192), V(as_, K, 192), V("at"))
         send(t, 1)
         act(V("a32"), V("at", 0, 4 * K), ACT.Identity, scale=32.0)
         if last:
             ts(V("cm", C + 1, E + 1), V("fl", C, E), -1025.0, 1024.0, A.mult, A.add)
-            tt(V(XN, 0, 2 * C), V("fo", 0, 2 * C), V("hm", 0, 2 * C), A.add)
+            tt(V(XN, 0, C), V("fo", 0, C), V("hm", 0, C), A.add)
             scan(V("mu", C, E), V("cm", C, E), V("bend", C, E), V("mu", C - 1, C), A.add, A.min)
-            tt(V(XN, 2 * C, 3 * C), V("fo", 2 * C, 3 * C), V("hm", 2 * C, 3 * C), A.add)
+            tt(V(XN, C, 2 * C), V("fo", C, 2 * C), V("hm", C, 2 * C), A.add)
             scan(V("muw", C, E), V("cmu", C, E), V("mu", C, E), 0.0, A.add, A.min)
-            tt(V(XN, 3 * C, 4 * C), V("fo", 3 * C, 4 * C), V("hm", 3 * C, 4 * C), A.add)
+            tt(V(XN, 2 * C, 3 * C), V("fo", 2 * C, 3 * C), V("hm", 2 * C, 3 * C), A.add)
             ts(V("muo", C // 16, E // 16), V("muw", C + 15, E, 16), OFW, None, A.add)
+            tt(V(XN, 3 * C, 4 * C), V("fo", 3 * C, 4 * C), V("hm", 3 * C, 4 * C), A.add)
             act(V("mr", C, E), ind(V("orr"), V("muo", C // 16, E // 16)), ACT.Copy)
             fin.append(dma("s", T.lm[:], T.mr[0:128:16, :], [V("mr")], []))
         else:
             tt(V(XN), V("fo"), V("hm"), A.add)
             quant(V("vq"), V("vs"), V("vt"))
         for b in range(4):
-            mm(V("d%d" % b, 0, 128), V("wq", 128 * b, 128 * b + 128), V("wp", 128 * b, 128 * b + 128), V(aq, 0, 128), V(as_, 0, 128))
+            mm(V(FB[b], 0, 128), V("wq", 128 * b, 128 * b + 128), V("wp", 128 * b, 128 * b + 128), V(aq, 0, 128), V(as_, 0, 128))
         for b in range(4):
-            tt(V("n32", b, 4 * K, 4), V("d%d" % b, 0, K), V("a32", b, 4 * K, 4), A.add, grp=("n32", t))
+            tt(V("n32", b, 4 * K, 4), V(FB[b], 0, K), V("a32", b, 4 * K, 4), A.add, grp=("n32", t))
         ts(V("nw"), V("n32"), 0.03125, None, A.mult)
         cp(ind(V(XN), V("evo")), V("nw"))
 
@@ -534,11 +631,12 @@ def rank_program(g, core, T, topo):
     quant(V(q, 0, hc), V(s, 0, hc), V("x%d" % R, 0, 4 * hc))
     quant(V(q, hc, C), V(s, hc, C), V("x%d" % R, 4 * hc, 4 * C))
     mm(V("pa", 0, hc), V("vq"), V("vs"), V(q, 0, hc), V(s, 0, hc))
-    mm(V("pb", 0, hc), V("vq"), V("vs"), V(q, hc, C), V(s, hc, C))
+    mm(V("pd", 0, hc), V("vq"), V("vs"), V(q, hc, C), V(s, hc, C))
     act(V("yo", 0, hc), V("pa", 0, hc), ACT.Copy)
-    cp(V("yo", hc, C), V("pb", 0, hc))
+    cp(V("yo", hc, C), V("pd", 0, hc))
     fin.append(dma("s", T.oc[:], T[q][:, 0:C].bitcast(dt.uint8), [V(q, 0, C)], [], grp="outs"))
-    fin.append(dma("a", T.y[:], T.yo[:], [V("yo")], []))
+    fin.append(dma("a", T.y[:, 0:hc], T.yo[:, 0:hc], [V("yo", 0, hc)], []))
+    fin.append(dma("a", T.y[:, hc:C], T.yo[:, hc:C], [V("yo", hc, C)], []))
     for k in range(4):
         fin.append(dma("s", T.osc[4 * k:4 * k + 4, :], T[s][32 * k:32 * k + 4, 0:C], [V(s, 0, C)], [], grp="outs"))
     ops.append({"q": "g", "fn": None, "deps": set(fin), "ev": ("end",), "inc": 0, "fixed": None})

@@ -10,38 +10,48 @@ def sb(n, d):
 
 
 TILES = [(24, 17, 16, 15), (14, 13, 8, 7), (12, 11, 10, 9), (6, 5, 4, 3), (23, 22, 21, 20), (19, 18, 2, 1)]
-WIDE = [max(128, 16 * max(c)) for c in TILES]
-BASE = [sum(WIDE[:c]) for c in range(len(TILES))]
-TW = sum(WIDE)
+WIDE = [C, 224, 192, 128, 368, E]
+ROOM = [C, 224, 192, E, 368, E]
+BASE = [sum(ROOM[:c]) for c in range(len(TILES))]
+TW = sum(ROOM)
 OWNV = 10
 HALOV = 20
-RRV = 4
+JW = 320
+SCUT = (288, 224, 128, 0)
+FCUT = (30, 36, 96)
+EARLY = 6
+SPLIT = 1
+FLK = -1
+CMK = 19
+ZD = 768
+HCUT = (62, 68, 72)
+NFL = (1, 2)
 KCUT = 144
-PCUT = (0, 6, 14, 24)
+PCUT = (0, 10, 20, 24)
 
 SCRATCH = {
     "ut": sb(512, BF), "vt": sb(512, BF), "uq": sb(128, X4), "us": sb(128, U8), "urq": sb(128, X4), "urs": sb(128, U8),
     "vq": sb(128, X4), "vs": sb(128, U8), "wq": sb(512, X4), "wp": sb(512, U8),
-    "ci": sb(8, I32), "cf": sb(16, F32), "expi": sb(8, I32), "t16": sb(E, BF), "tt": sb(E, F32), "zs": sb(E, BF),
+    "ci": sb(8, I32), "cf": sb(16, F32), "expi": sb(8, I32), "t16": sb(E, BF), "tt": sb(E, F32), "zs": sb(512, BF),
     "pku": sb(8, U16), "rgi": sb(4, F32), "rgo": sb(2, U16), "posc": sb(24, F32), "ygf": sb(24, F32), "ygo": sb(24, U16),
     "maskw": sb(E, BF), "capw": sb(E, BF), "rstw": sb(E, BF), "segr": sb(608, BF), "rst32": sb(768, BF), "c32": sb(E, BF),
-    "cmu": sb(E, BF), "cv": sb(C, F32), "d0k": sb(448, F32), "d0w": sb(24, F32), "ycw": sb(24, F32), "negt": sb(C, F32),
+    "cmu": sb(E, BF), "cv": sb(E, BF), "d0k": sb(448, F32), "d0w": sb(24, F32), "ycw": sb(30, F32), "negt": sb(C, F32),
     "cs": sb(8, F32), "ones": sb(512, BF), "et": sb(2048, BF), "eq": sb(512, X4), "es": sb(512, U8),
     "g1": sb(128, BF), "gt": sb(512, BF), "gq": sb(128, X4), "gs": sb(128, U8), "kc": sb(80, F32),
     "mm": sb(E, F32), "sc": sb(E, F32), "ta": sb(4 * TW, BF), "ca": sb(TW, X4), "sa": sb(TW, U8),
-    "rd": sb(E, BF), "rdc": sb(24, F32), "jv": sb(21 * 320, BF),
+    "rd": sb(E, BF), "rdc": sb(24, F32), "jv": sb(23 * JW, BF),
     "rs": sb(24, F32), "rr": sb(E, F32), "ext": sb(E, BF), "bz": sb(768, BF), "bh": sb(768, BF), "bt": sb(768, BF),
     "yb": sb(E, BF), "kr": sb(416, F32), "kw": sb(24, F32), "junk": sb(24 * 36, BF), "sg": sb(24, F32), "p2": sb(24, F32), "pso": sb(24, U16),
     "cmx": sb(E, BF), "smn": sb(E + 16, BF), "df": sb(E, BF), "fl": sb(E, BF), "bend": sb(E, F32), "cm": sb(E + 16, BF), "mu": sb(E, F32),
     "muw": sb(E, F32), "muo": sb(24, U16),
-    "orr": sb(E, F32), "mr": sb(E, F32), "ov": sb(C, F32), "mv": sb(C, F32), "ovo": sb(72, U16), "mvo": sb(72, U16),
-    "ft": sb(4 * E, BF), "fo": sb(4 * C, BF), "hm": sb(4 * C, BF),
-    "dd": sb(C, BF), "da": sb(C, BF), "jk2": sb(C, BF), "sv": sb(1, F32), "ii": sb(C, F32), "gg": sb(C + 16, BF), "xp": sb(320, BF),
+    "orr": sb(E, F32), "mr": sb(E, F32), "ov": sb(E, F32), "mv": sb(C, F32), "ovo": sb(96, U16), "mvo": sb(72, U16),
+    "ft": sb(4 * E, BF), "nw": sb(4 * K, BF), "hm": sb(4 * C, BF),
+    "dd": sb(C, BF), "da": sb(C, BF), "jk2": sb(C, BF), "sv": sb(1, F32), "ii": sb(C + 1, F32), "gg": sb(C + 16, BF), "xp": sb(320, BF),
     "tr": sb(608, BF), "sgm": sb(608, BF), "rko": sb(32, U16), "er": sb(C, F32), "ev": sb(K, F32), "evo": sb(16, U16),
-    "t1": sb(4 * K, BF), "t2": sb(4 * K, BF), "at": sb(512, BF), "a32": sb(4 * K, BF), "n32": sb(4 * K, BF), "nw": sb(4 * K, BF), "yo": sb(C, F32),
+    "t1": sb(4 * K, BF), "t2": sb(4 * K, BF), "at": sb(512, BF), "a32": sb(4 * K, BF), "n32": sb(4 * K, BF), "yo": sb(C, F32),
 }
 for _t in range(R + 1):
-    SCRATCH["x%d" % _t] = sb(4 * C, BF)
+    SCRATCH["x%d" % _t] = sb(4 * E, BF)
     SCRATCH["q%d" % _t] = sb(E, X4)
     SCRATCH["s%d" % _t] = sb(E, U8)
 for _t in range(R):
@@ -291,10 +301,12 @@ def rank_program(g, core, T, topo):
     RC, R4, B4, PR, GP, GI, YC, OFW, OFV, NV, RG, R33, YG, PR2, NG = [V("cf", i, i + 1) for i in range(15)]
 
     dma("s", T.x0[:, 0:512], T.x[:, 0:512], [], [V("x0", 0, 512)])
-    dma("a", T.ut[:], T.u[:], [], [V("ut")])
+    dma("s", T.ut[:], T.u[:], [], [V("ut")])
     dma("s", T.x0[:, 512:4 * C], T.x[:, 512:4 * C], [], [V("x0", 512, 4 * C)])
 
     def slot(k, lo, hi):
+        if k == 24 and lo >= C:
+            k = 2
         c = [k in tile for tile in TILES].index(True)
         e = TILES[c].index(k)
         return V("ta", 4 * (BASE[c] + lo) + e, 4 * (BASE[c] + hi), 4)
@@ -308,62 +320,74 @@ def rank_program(g, core, T, topo):
     iota(V("expi"), [[16, 8]], 0, 0, False)
     iota(V("kc", 0, 24), [[16, 24]], 0)
     iota(V("kc", 24, 52), [[-32, 7], [-16, 4]], 17)
-    iota(V("g1"), [[1, 8], [0, 16]], 0)
     zero(V("zs"))
-    hole(1)
     ts(V("ci", 0, 1), P, 15, None, A.bitwise_and, grp="ci")
+    ts(V("ci", 4, 5), P, 4, 1, A.arith_shift_right, A.bitwise_and, grp="ci")
     ts(V("ci", 1, 2), P, 2, 3, A.arith_shift_right, A.bitwise_and, grp="ci")
     ts(V("ci", 2, 3), P, 3, None, A.bitwise_and, grp="ci")
-    ts(V("ci", 4, 5), P, 4, 1, A.arith_shift_right, A.bitwise_and, grp="ci")
     ts(V("ci", 5, 6), P, 4, None, A.arith_shift_right, grp="ci")
-    hole(2)
     tt(V("ci", 6, 7), V("ci", 0, 1), V("ci", 4, 5), A.add)
+    cp(RC, V("ci", 0, 1))
     hole(3)
     ts(V("ci", 3, 4), V("ci", 6, 7), 1, None, A.bitwise_and)
-    hole(4)
-    cp(V("cf", 0, 6), V("ci", 0, 6))
-    hole(0)
+    hole(1)
     ts(V("maskw"), V("t16"), RC, None, A.is_equal)
-    ts(V("cs", 0, 4), V("t16", 0, 4), R4, 8704.0, A.is_equal, A.mult)
+    cp(V("cf", 1, 6), V("ci", 1, 6))
     cp(V("pku"), V("expi"))
-    fill(V("ones", 0, E), E, 1.0, "ones")
-    fill(V("ones", E, 512), 512 - E, 1.0, "ones")
+    fill(V("bz", 0, E), E, -1024.0)
+    fill(V("bz", E, 2 * E), E, -1024.0)
     act(V("rstw"), V("t16"), ACT.Identity, bias=-BIG, scale=2 * BIG)
+    act(V("capw"), V("maskw"), ACT.Identity, bias=-BIG, scale=2 * BIG)
     act(OFW, RC, ACT.Identity, bias=7680.0, scale=-512.0, grp="pad0")
     act(R33, RC, ACT.Identity, bias=6400.0 - 7680.0, scale=545.0, grp="pad0")
     act(YG, GP, ACT.Identity, bias=RC, scale=16.0, grp="pad0")
     act(PR2, PR, ACT.Identity, bias=15.0, scale=304.0, grp="pad0")
     act(RG, R4, ACT.Identity, bias=B4, scale=-2048.0, grp="pad0")
-    fill(V("rs", 0, 1), 1, 0.0, "pad")
-    act(V("ycw"), V("kc", 26, 50), ACT.Identity, bias=RC, grp="pad")
-    act(V("cs", 4, 8), V("cs", 0, 4), ACT.Identity, bias=-512.0, grp="pad")
+    fill(V("jv", JW - 1, JW), 1, 0.0, "pad")
+    act(V("ycw", 0, 24), V("kc", 26, 50), ACT.Identity, bias=RC, grp="pad")
     act(V("ygf"), V("kc", 0, 24), ACT.Identity, bias=YG, scale=2.0, grp="pad2")
-    act(V("capw"), V("maskw"), ACT.Identity, bias=-BIG, scale=2 * BIG)
+
+    def consts_act1():
+        act(V("ycw", 18, HALOV + 1), V("ycw", 18, HALOV + 1), ACT.Identity, bias=128.0)
+        for k in TILES[5]:
+            hi = C if k == 2 else E
+            fill(slot(k, 16 * k, hi), hi - 16 * k, 0.0)
 
     def consts_v1():
+        zero(V("ones"), c=1.0)
+        for lo in (128, 256):
+            quant(V("ca", BASE[3] + lo, BASE[3] + lo + 128), V("sa", BASE[3] + lo, BASE[3] + lo + 128), V("zs"))
+
+    def consts_v2():
+        for e in range(4):
+            ts(V("gt", e, 512, 4), V("g1"), GI, None, A.is_equal, grp="gt")
         cp(V("ygo"), V("ygf"))
         ts(V("rgi", 0, 2), V("kc", 0, 2), RC, 16.0, A.add, A.mult)
-        for k in TILES[5][1:]:
-            zero(slot(k, 16 * k, WIDE[5]), "zero")
+        ts(V("cs", 0, 4), V("t16", 0, 4), R4, 8704.0, A.is_equal, A.mult)
+        quant(GQ, GS, V("gt"))
         ts(V("rgo"), V("rgi", 0, 2), PR2, 607.0, A.add, A.min)
-        zero(V("bz"), c=-1024.0)
-        zero(V("c32"), c=32.0)
 
     def consts_act2():
+        act(V("cs", 4, 8), V("cs", 0, 4), ACT.Identity, bias=-512.0, grp="pad")
+        fill(V("c32"), E, 32.0)
         act(V("cmu"), V("maskw"), ACT.Identity, bias=-512.0, scale=33280.0)
         fill(V("c32", 32, E, 64), 6, 64.0)
         act(V("d0w"), V("kc", 54, 78), ACT.Identity, bias=R33, grp="pad2")
         act(NV, RC, ACT.Identity, bias=-0.5, scale=-1.0, grp="pad2")
         act(OFV, RG, ACT.Identity, bias=6144.0, grp="pad2")
         fill(V("gg", 0, 1), 1, 1024.0)
+        fill(V("gg", 1, 2), 1, 0.0)
 
     def consts_act3():
         for s in range(4):
-            act(V("cv", s, C, 4), V("zs", 0, C // 4), ACT.Identity, bias=V("cs", 4 + s, 5 + s), grp="cv")
+            act(V("cv", s, E, 4), V("zs", 0, E // 4), ACT.Identity, bias=V("cs", 4 + s, 5 + s), grp="cv")
 
     def consts_g():
-        iota(V("rst32"), [[0, 24], [8192, 32]], -1024)
-        iota(V("kc", 52, 80), [[2144, 7], [528, 4]], -1056)
+        iota(V("g1"), [[1, 8], [0, 16]], 0)
+        for b in range(4):
+            asel(V("et", 512 * b, 512 * b + 512), V("ones"), [[-4, 128], [-1, 4]], A.is_equal, b, 4)
+            if b == 1:
+                iota(V("kc", 52, 80), [[2144, 7], [528, 4]], -1056)
         iota(V("d0k"), [[-2144, 7], [-33, 64]], 1056 - 6400)
         iota(V("tt"), [[1, E]], 0)
         iota(V("kr", 0, 16), [[0, 16]], 0)
@@ -371,13 +395,12 @@ def rank_program(g, core, T, topo):
         iota(V("smn", E, E + 16), [[0, 16]], 4096)
         iota(V("posc"), [[32, 24]], 15)
         iota(V("cm", 0, 1), [[0, 1]], 1024)
-        for b in range(4):
-            asel(V("et", 512 * b, 512 * b + 512), V("ones"), [[-4, 128], [-1, 4]], A.is_equal, b, 4)
         iota(V("negt"), [[-1, C]], 0)
         iota(V("xp", 0, 16), [[0, 16]], 0)
         iota(V("xp", 304, 320), [[0, 16]], 0)
         iota(V("segr"), [[0, 38], [4096, 16]], -2048)
         iota(V("at", 4 * K, 512), [[0, 4 * K]], 0)
+        dma("g", T.vt[:], T.v[:], [], [V("vt")])
 
     GQ, GS = V("gq"), V("gs")
     FB = ["d0", "d1", "d2", "pb"]
@@ -394,17 +417,21 @@ def rank_program(g, core, T, topo):
         quant(V(q, 0, 128), V(s, 0, 128), V(X, 0, 512))
         send(t, 0)
         if t == 0:
-            consts_g()
             dma("s", T.wq[:].bitcast(dt.uint8), T.wc[:], [V(q, C, E)], [V("wq")])
             dma("s", T.wp[:], T.ws[:], [], [V("wp")])
-            dma("s", T.vt[:], T.v[:], [], [V("vt")])
+            zero(V("rst32"), c=8192.0)
             quant(V("uq"), V("us"), V("ut"))
-        quant(V(q, 128, C), V(s, 128, C), V(X, 512, 4 * C))
-        if t == 0:
+            hole(0)
+            hole(2)
+            hole(4)
+            zero(V("rst32", 0, 768, 32), c=-1024.0)
             op("v", lambda: g.vector.tensor_copy(T.urq[:].bitcast(dt.uint32), T.uq[:].bitcast(dt.uint32).indirect(T.pku[:])), [V("uq"), V("pku")], [V("urq")])
             act(V("urs"), ind(V("us"), V("pku")), ACT.Copy)
-            for e in range(4):
-                ts(V("gt", e, 512, 4), V("g1"), GI, None, A.is_equal, grp="gt")
+        quant(V(q, 128, C), V(s, 128, C), V(X, 512, 4 * C))
+        if t == 0:
+            consts_v1()
+            consts_act1()
+            consts_g()
 
         def score(bank, lo, hi):
             mm(V(bank, 0, hi - lo), V("urq"), V("urs"), V(q, lo, hi), V(s, lo, hi))
@@ -412,11 +439,11 @@ def rank_program(g, core, T, topo):
         def hold(lo, hi):
             scan(V("sc", lo, hi), V("rstw", lo, hi), V("mm", lo, hi), 0.0, A.min, A.max)
 
-        def cmp_v(k, grp=None):
-            ts(slot(k, 0, min(C, 16 * k)), V("pa", 0, min(C, 16 * k)), sw(k), None, A.is_lt, grp=grp)
+        def cmp_v(k, bank="pa"):
+            ts(slot(k, 0, min(C, 16 * k)), V(bank, 0, min(C, 16 * k)), sw(k), None, A.is_lt)
 
         def count_v(k, grp=None):
-            scan(V("jv", 320 * k + 320 - 16 * k, 320 * k + 320), slot(k, 0, 16 * k), V("zs", 0, 16 * k), -128.0, A.add, A.add, grp=grp)
+            scan(V("jv", JW * k + JW - 16 * k, JW * k + JW), slot(k, 0, 16 * k), V("zs", 0, 16 * k), -128.0 if k > 16 else 0.0, A.add, A.add)
 
         def runs(lo, hi):
             scan(V("rd", lo, hi), V("t16", lo, hi), slot(24, lo, hi), 0.0, A.min, A.add)
@@ -431,25 +458,27 @@ def rank_program(g, core, T, topo):
                 act(slot(k, 0, 16 * k), slot(k, 0, 16 * k), ACT.Relu, accum=V("rs", k, k + 1), grp=grp)
 
         def na(c, first=False, end=False):
-            w = WIDE[c]
+            w = ROOM[c]
             mm(V("na", 0, w), GQ, GS, V("ca", BASE[c], BASE[c] + w), V("sa", BASE[c], BASE[c] + w), first, end, grp=("na", t))
 
-        def unpack(b):
-            mm(V(FB[b], 0, E), V("eq", 128 * b, 128 * b + 128), V("es", 128 * b, 128 * b + 128), V(q, 0, E), V(s, 0, E))
-            act(V("ft", b, 4 * E, 4), V(FB[b], 0, E), ACT.Copy)
+        def unpack(b, product=True, copy=True):
+            if product:
+                mm(V(FB[b], 0, E), V("eq", 128 * b, 128 * b + 128), V("es", 128 * b, 128 * b + 128), V(q, 0, E), V(s, 0, E))
+            if copy:
+                act(V("ft", b, 4 * E, 4), V(FB[b], 0, E), ACT.Copy)
 
         def pack_e(b):
             quant(V("eq", 128 * b, 128 * b + 128), V("es", 128 * b, 128 * b + 128), V("et", 512 * b, 512 * b + 512))
 
         score("pa", 0, C)
         score("pb", 0, C)
-        cut = 208
-        tt(V("mm", cut, C), V("pa", cut, C), V("capw", cut, C), A.min)
-        tt(V("mm", 0, cut), V("pa", 0, cut), V("capw", 0, cut), A.min)
-        hold(cut, C)
-        hold(0, cut)
+        cuts = list(zip(SCUT[1:], SCUT[:-1]))
+        for lo, hi in cuts:
+            tt(V("mm", lo, hi), V("pa", lo, hi), V("capw", lo, hi), A.min)
+        for lo, hi in cuts:
+            hold(lo, hi)
         both((17, 16, 15), "pb", ("both", t, 0))
-        both((14, 13, 12, 11), "pb", ("both", t, 1))
+        both(range(14, OWNV, -1), "pb", ("both", t, 1))
         for k in range(OWNV, OWNV - 3, -1):
             cmp_v(k)
         tt(slot(24, 0, C), V("pa", 0, C), V("sc", 0, C), A.is_le)
@@ -460,11 +489,12 @@ def rank_program(g, core, T, topo):
             count_v(k)
         tt(V("rdc", 0, 18), V("rd", 15, C, 16), V("ycw", 0, 18), A.add)
         qa(3, 0, WIDE[3])
-        ts(V("rs", 1, OWNV + 1), V("jv", 639, 320 * (OWNV + 1), 320), 128.0, None, A.add)
 
         def counts(step, lo, hi):
             if step == 0:
                 tt(V("bz", 32 * lo, 32 * hi, 32), V("rdc", lo, hi), V("rs", lo, hi), A.add)
+            elif step == 5:
+                tt(V("bz", 32 * lo, 32 * hi, 32), V("rdc", lo, hi), V("jv", JW * lo + JW - 1, JW * hi, JW), A.add)
             elif step == 1:
                 scan(V("bh", 32 * lo, 32 * hi), V("rst32", 32 * lo, 32 * hi), V("bz", 32 * lo, 32 * hi), 0.0, A.min, A.max)
             elif step == 2:
@@ -474,76 +504,88 @@ def rank_program(g, core, T, topo):
             else:
                 act(V("rr", 16 * lo, 16 * hi), ind(V("bt", 0, 32 * hi), V("ygo", lo, hi)), ACT.Identity, bias=6159.5)
 
+        steps = [lambda: qa(0, 0, WIDE[0]), lambda: counts(5, 0, OWNV + 1), lambda: counts(0, OWNV + 1, 18), lambda: qa(1, 0, WIDE[1]),
+                 lambda: counts(1, 0, 18), lambda: qa(2, 0, WIDE[2]), lambda: counts(2, 0, 18), lambda: counts(4, 0, 18)]
+        early = EARLY if t == 0 else 1
+
+        def step(i):
+            if i >= early:
+                steps[i]()
+
+        for i in range(early):
+            steps[i]()
+            if i == 1 and t == 0:
+                consts_v2()
+            if i in (3, 4, 5):
+                pack_e(i - 3)
         if t == 0:
-            consts_v1()
-            quant(GQ, GS, V("gt"))
-            qa(0, 0, 256)
-            counts(0, 0, 18)
-            qa(1, 0, WIDE[1])
-            counts(1, 0, 18)
-            qa(2, 0, WIDE[2])
-            counts(2, 0, 18)
-            counts(4, 0, 18)
+            consts_act2()
+            consts_act3()
         score("ph", 256, E)
         score("pd", 0, E)
         tt(V("mm", C, E), V("ph", C - 256, 128), V("capw", C, E), A.min)
-        if t > 0:
-            qa(0, 0, 256)
+        step(1)
+        na(3, True)
+        na(0)
         hold(C, E)
-        if t > 0:
-            counts(0, 0, 18)
-            qa(1, 0, WIDE[1])
-            counts(1, 0, 18)
+        step(3)
+        na(1)
         both(range(23, HALOV, -1), "pd", ("both", t, 2))
         for k in range(HALOV, 18, -1):
             ts(slot(k, C, 16 * k), V("ph", C - 256, 16 * k - 256), sw(k), None, A.is_lt)
         tt(slot(24, C, E), V("ph", C - 256, 128), V("sc", C, E), A.is_le)
-        if t > 0:
-            counts(2, 0, 18)
         cmp_v(19)
         runs(C, E)
+        step(2)
         cmp_v(18)
-        qa(0, 256, E)
-        if HALOV > 19:
-            cmp_v(20)
+        step(4)
+        for k in range(20, HALOV + 1):
+            cmp_v(k)
+        step(6)
+        step(7)
+        for b in range(2 if t == 0 else 4):
+            unpack(b, True, b < 2)
         tt(V("rdc", 18, 24), V("rd", C + 15, E, 16), V("ycw", 18, 24), A.add)
         for k in range(18, HALOV + 1):
             count_v(k)
-        if t > 0:
-            qa(2, 0, WIDE[2])
-            counts(RRV, 0, 18)
-        ts(V("rs", 18, HALOV + 1), V("jv", 320 * 18 + 319, 320 * (HALOV + 1), 320), 128.0, None, A.add)
         qa(5, 0, WIDE[5])
-        counts(0, 18, 24)
-        qa(4, 0, 192)
+        counts(0, HALOV + 1, 24)
+        counts(5, 18, HALOV + 1)
+        qa(4, 0, WIDE[4])
         counts(1, 18, 24)
-        qa(4, 192, WIDE[4])
+        step(5)
         counts(2, 18, 24)
+        counts(4, 18, 24)
         if t == 0:
-            pack_e(0)
-        counts(3, 18, 24)
+            pack_e(3)
 
-        for c in (0, 1, 3, 2, 5, 4):
-            na(c, c == 0, c == 4)
-        if t == 0:
-            consts_act2()
-        else:
-            for b in range(3):
-                unpack(b)
-        tt(V("yb"), V("rr"), V("na", 0, E), A.subtract)
-        if t == 0:
-            pack_e(1)
-        scan(V("ext"), V("cmu"), V("yb"), 0.0, A.add, A.min)
-        scan(V("kr", 16, 16 + KCUT), V("d0k", 32, 32 + KCUT), V("yb", 0, KCUT), 0.0, A.min, A.add)
-        scan(V("cmx"), V("c32"), V("yb"), 8192.0, A.add, A.min)
-        tt(V("kw"), V("d0w"), V("ext", 15, E, 16), A.subtract)
-        scan(V("kr", 16 + KCUT, 16 + E), V("d0k", 32 + KCUT, 32 + E), V("yb", KCUT, E), 0.0, A.min, A.add)
+        order = (5, 4, 2) if t > 0 else (2, 5, 4)
+        for c in order:
+            na(c, False, c == order[-1])
+        for b in range(2, 2 + NFL[t > 0]):
+            unpack(b, t == 0)
+        for lo, hi in ((0, KCUT), (KCUT, E)):
+            tt(V("yb", lo, hi), V("rr", lo, hi), V("na", lo, hi), A.subtract)
+        for lo, hi in ((0, KCUT), (KCUT, E)):
+            scan(V("ext", lo, hi), V("cmu", lo, hi), V("yb", lo, hi), 0.0, A.add, A.min)
+            scan(V("kr", 16 + lo, 16 + hi), V("d0k", 32 + lo, 32 + hi), V("yb", lo, hi), 0.0, A.min, A.add)
+            if lo == 0:
+                scan(V("cmx"), V("c32"), V("yb"), 8192.0, A.add, A.min)
+            else:
+                scan(V("df"), V("smn", 1, E + 1), V("cmx"), 0.0, A.max, A.subtract)
+            tt(V("kw", lo // 16, hi // 16), V("d0w", lo // 16, hi // 16), V("ext", lo + 15, hi, 16), A.subtract)
+            if lo == 0:
+                scan(V("smn", E - 1, None, -1), V("yb", E - 1, None, -1), V("c32", E - 1, None, -1), 0.0, A.max, A.subtract)
         for k in range(24):
             act(V("junk", 36 * k, 36 * k + 36), V("kr", 6 + 16 * k, 42 + 16 * k), ACT.Sign, bias=V("kw", k, k + 1), accum=V("sg", k, k + 1))
-        if t == 0:
-            consts_act3()
-        else:
-            unpack(3)
+            if k == FLK:
+                act(V("fl"), V("df"), ACT.Sign)
+            if k == CMK:
+                if FLK < 0:
+                    ts(V("fl"), V("df"), 0.0, None, A.is_gt)
+                act(V("cm", 1, E + 1 if last else C + 1), V("fl", 0, E if last else C), ACT.Identity, scale=-1025.0, bias=1024.0)
+        for b in range(2 + NFL[t > 0], 4):
+            unpack(b, t == 0)
 
         def position(step, h):
             lo, hi = PCUT[h], PCUT[h + 1]
@@ -554,77 +596,114 @@ def rank_program(g, core, T, topo):
             else:
                 cp(ind(V("orr"), V("pso", lo, hi)), V("tt", 16 * lo, 16 * hi))
 
-        scan(V("smn", E - 1, None, -1), V("yb", E - 1, None, -1), V("c32", E - 1, None, -1), 0.0, A.max, A.subtract)
-        if t == 0:
-            pack_e(2)
-        scan(V("df"), V("smn", 1, E + 1), V("cmx"), 0.0, A.max, A.subtract)
-        if t == 0:
-            pack_e(3)
-            for b in range(4):
-                unpack(b)
         position(0, 0)
-        ts(V("fl"), V("df"), 0.0, None, A.is_gt)
+        scan(V("bend", E - 1, None, -1), V("fl", E - 1, None, -1), V("tt", E - 1, None, -1), 0.0, A.mult, A.max)
         position(1, 0)
-        ts(V("cm", 1, C + 1), V("fl", 0, C), -1025.0, 1024.0, A.mult, A.add)
+
+        JC = 16 * PCUT[1] - 16
+
+        def far(step, lo, hi):
+            if step == 0:
+                scan(V("dd", lo, hi), V("negt", lo, hi), V("orr", lo, hi), 0.0, A.min, A.add)
+                act(V("da", lo, hi), V("dd", lo, hi), ACT.Abs)
+            elif step == 1:
+                act(V("jk2", lo, hi), V("da", lo, hi), ACT.Sign, bias=NV, accum=V("sv") if lo == 0 else V("ii", 0, 1))
+            elif step == 2:
+                ts(V("ii", lo + 1, hi + 1), V("da", lo, hi), RC, 1026.0, A.is_equal, A.mult)
+            elif step == 3:
+                ts(V("gg", lo + 2, hi + 2), V("da", lo, hi), RC, 1024.0, A.is_equal, A.mult)
+            elif step == 4:
+                scan(V("ov", lo, hi), V("cv", lo, hi), V("orr", lo, hi), 0.0, A.add, A.min)
+            else:
+                ts(V("ovo", lo // 4, hi // 4), V("ov", lo + 3, hi, 4), 4.0, OFV, A.mult, A.add)
+
+        def gather_o(lo, hi):
+            act(V(XN, 16 * lo, 16 * hi), ind(V("ft"), V("ovo", lo, hi)), ACT.Copy)
+
         position(2, 0)
         position(0, 1)
-        scan(V("bend", E - 1, None, -1), V("fl", E - 1, None, -1), V("tt", E - 1, None, -1), 0.0, A.mult, A.max)
+        far(4, 0, JC)
         position(1, 1)
-        position(0, 2)
+        if SPLIT:
+            far(0, 0, JC)
+        far(5, 0, JC)
+        if SPLIT:
+            far(1, 0, JC)
+        gather_o(0, FCUT[0])
         scan(V("mu", 0, C), V("cm", 0, C), V("bend", 0, C), 0.0, A.add, A.min)
         position(2, 1)
+        position(0, 2)
+        lo = JC if SPLIT else 0
+        if SPLIT:
+            far(2, 0, JC)
         position(1, 2)
-        scan(V("muw", 0, C), V("cmu", 0, C), V("mu", 0, C), 0.0, A.add, A.min)
+        far(0, lo, C)
+        if SPLIT:
+            far(3, 0, JC)
+        JD = 16 * PCUT[2] - 16
+        far(4, JC, JD)
         position(2, 2)
-        ts(V("muo", 0, C // 16), V("muw", 15, C, 16), OFW, None, A.add)
-        scan(V("dd"), V("negt"), V("orr", 0, C), 0.0, A.min, A.add)
-        scan(V("ov"), V("cv"), V("orr", 0, C), 0.0, A.add, A.min)
-        act(V("mr", 0, C), ind(V("orr"), V("muo", 0, C // 16)), ACT.Copy)
-        act(V("da"), V("dd"), ACT.Abs)
-        act(V("jk2"), V("da"), ACT.Sign, bias=NV, accum=V("sv"))
-        ts(V("ovo"), V("ov", 3, C, 4), 4.0, OFV, A.mult, A.add)
-        scan(V("mv"), V("cv"), V("mr", 0, C), 0.0, A.add, A.min)
-        act(V("fo"), ind(V("ft"), V("ovo")), ACT.Copy)
-        ts(V("gg", 1, C + 1), V("da"), RC, 1024.0, A.is_equal, A.mult)
-        ts(V("mvo"), V("mv", 3, C, 4), 4.0, OFV, A.mult, A.add)
-        ts(V("ii"), V("da"), RC, 1026.0, A.is_equal, A.mult)
-        act(V("hm"), ind(V("ft"), V("mvo")), ACT.Identity, scale=-0.5)
-        scan(V("xp", 16, 304), V("ii"), V("gg", 0, C), V("sv"), A.add, A.subtract)
+        far(5, JC, JD)
+        gather_o(FCUT[0], FCUT[1])
+        far(1, lo, C)
+        gather_o(FCUT[1], JD // 4)
+        far(2, lo, C)
+        far(3, lo, C)
+        far(4, JD, E)
+        if SPLIT:
+            scan(V("xp", 15, 304), V("ii"), V("gg", 0, C + 1), V("sv"), A.add, A.subtract)
+        else:
+            scan(V("xp", 16, 304), V("ii", 1, C + 1), V("gg", 1, C + 1), V("sv"), A.add, A.subtract)
+        far(5, JD, E)
+        if FCUT[2] > JD // 4:
+            gather_o(JD // 4, FCUT[2])
+        scan(V("mv"), V("cv", 0, C), V("mu", 0, C), 0.0, A.add, A.min)
         trp(V("tr", 0, C), V("xp", 16, 304))
         trp(V("tr", C, 608), V("xp"))
+        ts(V("mvo"), V("mv", 3, C, 4), 4.0, OFV, A.mult, A.add)
         scan(V("sgm", 0, C), V("segr", 0, C), V("tr", 0, C), 0.0, A.min, A.max)
         scan(V("sgm", C, 608), V("segr", C, 608), V("tr", C, 608), 0.0, A.min, A.max)
+        if FCUT[2] < 96:
+            cp(V(XN, 16 * FCUT[2], 4 * E), ind(V("ft"), V("ovo", FCUT[2], 96)))
+        act(V("hm", 0, 16 * HCUT[0]), ind(V(XN), V("mvo", 0, HCUT[0])), ACT.Identity, scale=-0.5)
         ts(V("rko"), ind(V("sgm"), V("rgo")), 0.5, 143.0, A.mult, A.add)
         cp(ind(V("er"), V("rko", 0, 18)), V("tt", 0, C))
+
+        def gather_m(h):
+            if HCUT[h + 1] > HCUT[h]:
+                ts(V("hm", 16 * HCUT[h], 16 * HCUT[h + 1]), ind(V(XN), V("mvo", HCUT[h], HCUT[h + 1])), -0.5, None, A.mult)
+
+        gather_m(0)
         scan(V("ev"), V("cv", 0, K), V("er", 0, K), 0.0, A.add, A.min)
+        gather_m(1)
         ts(V("evo"), V("ev", 3, K, 4), 4.0, OFV, A.mult, A.add)
-        cp(V("t2"), ind(V("fo"), V("evo")))
+        if last:
+            scan(V("mu", C, E), V("cm", C, E), V("bend", C, E), V("mu", C - 1, C), A.add, A.min)
+        for h in range(2):
+            cp(V("t2", 128 * h, 128 * h + 128), ind(V(XN, 0, 4 * C), V("evo", 8 * h, 8 * h + 8)))
         for h in range(2):
             act(V("t1", 128 * h, 128 * h + 128), ind(V("hm"), V("evo", 8 * h, 8 * h + 8)), ACT.Copy)
             tt(V("at", 128 * h, 128 * h + 128), V("t1", 128 * h, 128 * h + 128), V("t2", 128 * h, 128 * h + 128), A.add)
         quant(V(aq, K, 192), V(as_, K, 192), V("at"))
         send(t, 1)
+        op("g", lambda XN=XN: g.dma_start(T[XN][:, ZD:4 * C], T.hm[:, ZD:4 * C], accum_op=A.add), [V("hm", ZD, 4 * C), V(XN, ZD, 4 * C)],
+           [V(XN, ZD, 4 * C)], inc=16)
         act(V("a32"), V("at", 0, 4 * K), ACT.Identity, scale=32.0)
         if last:
-            ts(V("cm", C + 1, E + 1), V("fl", C, E), -1025.0, 1024.0, A.mult, A.add)
-            tt(V(XN, 0, C), V("fo", 0, C), V("hm", 0, C), A.add)
-            scan(V("mu", C, E), V("cm", C, E), V("bend", C, E), V("mu", C - 1, C), A.add, A.min)
-            tt(V(XN, C, 2 * C), V("fo", C, 2 * C), V("hm", C, 2 * C), A.add)
-            scan(V("muw", C, E), V("cmu", C, E), V("mu", C, E), 0.0, A.add, A.min)
-            tt(V(XN, 2 * C, 3 * C), V("fo", 2 * C, 3 * C), V("hm", 2 * C, 3 * C), A.add)
-            ts(V("muo", C // 16, E // 16), V("muw", C + 15, E, 16), OFW, None, A.add)
-            tt(V(XN, 3 * C, 4 * C), V("fo", 3 * C, 4 * C), V("hm", 3 * C, 4 * C), A.add)
-            act(V("mr", C, E), ind(V("orr"), V("muo", C // 16, E // 16)), ACT.Copy)
-            fin.append(dma("s", T.lm[:], T.mr[0:128:16, :], [V("mr")], []))
+            scan(V("muw"), V("cmu"), V("mu"), 0.0, A.add, A.min)
+        tt(V(XN, 0, ZD), V(XN, 0, ZD), V("hm", 0, ZD), A.add)
+        if last:
+            ts(V("muo"), V("muw", 15, E, 16), OFW, None, A.add)
+            act(V("mr"), ind(V("orr"), V("muo")), ACT.Copy)
+            fin.append(dma("a", T.lm[:], T.mr[0:128:16, :], [V("mr")], []))
         else:
-            tt(V(XN), V("fo"), V("hm"), A.add)
             quant(V("vq"), V("vs"), V("vt"))
         for b in range(4):
             mm(V(FB[b], 0, 128), V("wq", 128 * b, 128 * b + 128), V("wp", 128 * b, 128 * b + 128), V(aq, 0, 128), V(as_, 0, 128))
         for b in range(4):
             tt(V("n32", b, 4 * K, 4), V(FB[b], 0, K), V("a32", b, 4 * K, 4), A.add, grp=("n32", t))
         ts(V("nw"), V("n32"), 0.03125, None, A.mult)
-        cp(ind(V(XN), V("evo")), V("nw"))
+        cp(ind(V(XN, 0, 4 * C), V("evo")), V("nw"))
 
     q, s = "q%d" % R, "s%d" % R
     hc = C // 2
@@ -635,8 +714,7 @@ def rank_program(g, core, T, topo):
     act(V("yo", 0, hc), V("pa", 0, hc), ACT.Copy)
     cp(V("yo", hc, C), V("pd", 0, hc))
     fin.append(dma("s", T.oc[:], T[q][:, 0:C].bitcast(dt.uint8), [V(q, 0, C)], [], grp="outs"))
-    fin.append(dma("a", T.y[:, 0:hc], T.yo[:, 0:hc], [V("yo", 0, hc)], []))
-    fin.append(dma("a", T.y[:, hc:C], T.yo[:, hc:C], [V("yo", hc, C)], []))
+    fin.append(dma("a", T.y[:], T.yo[:], [V("yo")], []))
     for k in range(4):
         fin.append(dma("s", T.osc[4 * k:4 * k + 4, :], T[s][32 * k:32 * k + 4, 0:C], [V(s, 0, C)], [], grp="outs"))
     ops.append({"q": "g", "fn": None, "deps": set(fin), "ev": ("end",), "inc": 0, "fixed": None})

import numpy as np
from concourse.mybir import dt, AluOpType, ActivationFunctionType

C, H, E, K, J, R = 288, 96, 384, 64, 3, 2
X4, U8, U16, BF, F32, I32 = "float8_e4m3fn_x4", "uint8", "uint16", "bfloat16", "float32", "int32"


def sb(n, d):
    return ("sbuf", [128, n], d)


TILES = [(24, 17, 16, 15), (14, 13, 8, 7), (12, 11, 10, 9), (6, 5, 4, 3), (23, 22, 21, 20), (19, 18, 2, 1)]
WIDE = [C, 224, 192, 128, 368, E]
ROOM = [C, 224, 192, E, 368, E]
BASE = [sum(ROOM[:c]) for c in range(len(TILES))]
TW = sum(ROOM)
OWNV = 10
HALOV = 20
JW = 320
SCUT = (288, 224, 128, 0)
FCUT = (30, 36, 96)
EARLY = 6
SPLIT = 1
FLK = -1
CMK = 19
ZD = 768
HCUT = (62, 68, 72)
NFL = (1, 2)
KCUT = 144
PCUT = (0, 10, 20, 24)

SCRATCH = {
    "ut": sb(512, BF), "vt": sb(512, BF), "uq": sb(128, X4), "us": sb(128, U8), "urq": sb(128, X4), "urs": sb(128, U8),
    "vq": sb(128, X4), "vs": sb(128, U8), "wq": sb(512, X4), "wp": sb(512, U8),
    "ci": sb(8, I32), "cf": sb(16, F32), "expi": sb(8, I32), "t16": sb(E, BF), "tt": sb(E, F32), "zs": sb(512, BF),
    "pku": sb(8, U16), "rgi": sb(4, F32), "rgo": sb(2, U16), "posc": sb(24, F32), "ygf": sb(24, F32), "ygo": sb(24, U16),
    "maskw": sb(E, BF), "capw": sb(E, BF), "rstw": sb(E, BF), "segr": sb(608, BF), "rst32": sb(768, BF), "c32": sb(E, BF),
    "cmu": sb(E, BF), "cv": sb(E, BF), "d0k": sb(448, F32), "d0w": sb(24, F32), "ycw": sb(30, F32), "negt": sb(C, F32),
    "cs": sb(8, F32), "ones": sb(512, BF), "et": sb(2048, BF), "eq": sb(512, X4), "es": sb(512, U8),
    "g1": sb(128, BF), "gt": sb(512, BF), "gq": sb(128, X4), "gs": sb(128, U8), "kc": sb(80, F32),
    "mm": sb(E, F32), "sc": sb(E, F32), "ta": sb(4 * TW, BF), "ca": sb(TW, X4), "sa": sb(TW, U8),
    "rd": sb(E, BF), "rdc": sb(24, F32), "jv": sb(23 * JW, BF),
    "rs": sb(24, F32), "rr": sb(E, F32), "ext": sb(E, BF), "bz": sb(768, BF), "bh": sb(768, BF), "bt": sb(768, BF),
    "yb": sb(E, BF), "kr": sb(416, F32), "kw": sb(24, F32), "junk": sb(24 * 36, BF), "sg": sb(24, F32), "p2": sb(24, F32), "pso": sb(24, U16),
    "cmx": sb(E, BF), "smn": sb(E + 16, BF), "df": sb(E, BF), "fl": sb(E, BF), "bend": sb(E, F32), "cm": sb(E + 16, BF), "mu": sb(E, F32),
    "muw": sb(E, F32), "muo": sb(24, U16),
    "orr": sb(E, F32), "mr": sb(E, F32), "ov": sb(E, F32), "mv": sb(C, F32), "ovo": sb(96, U16), "mvo": sb(72, U16),
    "ft": sb(4 * E, BF), "nw": sb(4 * K, BF), "hm": sb(4 * C, BF),
    "dd": sb(C, BF), "da": sb(C, BF), "jk2": sb(C, BF), "sv": sb(1, F32), "ii": sb(C + 1, F32), "gg": sb(C + 16, BF), "xp": sb(320, BF),
    "tr": sb(608, BF), "sgm": sb(608, BF), "rko": sb(32, U16), "er": sb(C, F32), "ev": sb(K, F32), "evo": sb(16, U16),
    "t1": sb(4 * K, BF), "t2": sb(4 * K, BF), "at": sb(512, BF), "a32": sb(4 * K, BF), "n32": sb(4 * K, BF), "yo": sb(C, F32),
}
for _t in range(R + 1):
    SCRATCH["x%d" % _t] = sb(4 * E, BF)
    SCRATCH["q%d" % _t] = sb(E, X4)
    SCRATCH["s%d" % _t] = sb(E, U8)
for _t in range(R):
    SCRATCH["aq%d" % _t] = sb(192, X4)
    SCRATCH["as%d" % _t] = sb(192, U8)
BANKS = ["d0", "d1", "d2", "pa", "pb", "na", "ph", "pd"]
for _b in BANKS:
    SCRATCH[_b] = ("psum", [128, 512], F32)

NDMA = 12
SEMAPHORES = (["sent"] + ["h%d" % t for t in range(R)] + ["f%d" % t for t in range(R)] + ["e%d" % i for i in range(NDMA)]
              + ["c" + q for q in "vapg"])

A = AluOpType
ACT = ActivationFunctionType
BIG = 1e28


def routes(T, topo):
    n = len(T.cores)
    out = []
    for r in range(n):
        c = T.cores[r]
        dsts = [T.cores[(r - 1) % n], T.cores[(r + J) % n]]
        need = [not topo.may_write(c, d) for d in dsts]
        if not any(need):
            out.append((None, [False, False]))
            continue
        ok = [k for k in topo.cores_of(c) if k != c and T.rank_of(k) is None and all(topo.may_write(k, d) for d in dsts)]
        ok.sort(key=lambda k: (topo.die(k) != topo.die(c), k))
        out.append((ok[:2], [True, need[1]]))
    return out


def pieces(T, t, which):
    if which == 0:
        q, s = T["q%d" % t], T["s%d" % t]
        return [(q[:, 0:H].bitcast(dt.uint8), q[:, C:E].bitcast(dt.uint8)), (s[:, 0:H], s[:, C:E])]
    q, s = T["aq%d" % t], T["as%d" % t]
    return [(q[:, K:2 * K].bitcast(dt.uint8), q[:, 0:K].bitcast(dt.uint8)), (s[:, K:2 * K], s[:, 0:K])]


def relay_program(g, core, T, topo, r, part, via):
    n = len(T.cores)
    src = T.cores[r]
    sent = 0
    for t in range(R):
        for which in range(2):
            if not via[which]:
                continue
            dst = T.cores[(r - 1) % n] if which == 0 else T.cores[(r + J) % n]
            sem = T.sem["hf"[which] + str(t)]
            land = pieces(T, t, which)[part][1]
            g.wait_ge(sem, len(topo.engines(src, core)))
            rid, pid = topo.addr(dst, core)
            g.remote_dma(land, land, sem, T.sem.sent, pid, rid, topo.mask(core, dst))
            sent += len(topo.engines(core, dst))
    g.wait_ge(T.sem.sent, sent)


def rank_program(g, core, T, topo):
    rt = routes(T, topo)
    rank = T.rank_of(core)
    if rank is None:
        for r in range(len(T.cores)):
            if rt[r][0] is not None and core in rt[r][0]:
                relay_program(g, core, T, topo, r, rt[r][0].index(core), rt[r][1])
        return
    n = len(T.cores)
    Q = {"g": g, "v": g.vector, "a": g.scalar, "p": g.tensor, "s": g.sync}

    ops = []
    hist = {}

    def V(name, a=0, b=None, s=1):
        return (name, a, b, s)

    def ind(w, o):
        return ("ind", w, o)

    def ap(v):
        if not isinstance(v, tuple):
            return v
        if v[0] == "ind":
            return ap(v[1]).indirect(ap(v[2]))
        if v[3] == 1:
            return T[v[0]][:, v[1]:v[2]] if v[2] is not None else T[v[0]][:, v[1]:]
        return T[v[0]][:, v[1]:v[2]:v[3]]

    def flat(vs):
        out = []
        for v in vs:
            if isinstance(v, tuple):
                out += [v[1], v[2]] if v[0] == "ind" else [v]
        return out

    def op(q, fn, reads, writes, grp=None, inc=1, fixed=None, acc=False):
        me = len(ops)
        deps = set()
        rd = flat(reads) + [v[2] for v in writes if v[0] == "ind"]
        wr = [v[1] if v[0] == "ind" else v for v in writes]
        for isw, vs in ((False, rd), (True, wr)):
            for v in vs:
                w = SCRATCH[v[0]][1][1]
                psum = v[0] in BANKS
                m = np.zeros(w, bool)
                if psum:
                    m[:] = True
                else:
                    m[v[1]:v[2]:v[3]] = True
                h = hist.setdefault(v[0], [])
                keep = []
                for (o, ow, oq, om) in h:
                    hit = bool((om & m).any())
                    if o != me and hit and (isw or ow or (psum and oq != q)) and not (acc and oq == q and ow and psum):
                        deps.add(o)
                    if isw and hit and not acc:
                        om = om & ~m
                    if om.any():
                        keep.append((o, ow, oq, om))
                keep.append((me, isw, q, m))
                hist[v[0]] = keep
        ops.append({"q": q, "fn": fn, "deps": deps, "ev": grp if grp is not None else ("op", me), "inc": inc, "fixed": fixed})
        return me

    def emit():
        members = {}
        for i, o in enumerate(ops):
            members.setdefault(o["ev"], []).append(i)
        know = {q: 0 for q in Q}
        done = {q: 0 for q in Q}
        count = {q: 0 for q in Q}
        at = []
        where = {}
        ndma = [0]
        for i, o in enumerate(ops):
            q, ev = o["q"], o["ev"]
            if q is None:
                where[ev] = o["fixed"]
                at.append(1 << i)
                continue
            for d in sorted(o["deps"], reverse=True):
                if know[q] >> d & 1:
                    continue
                w = ops[d]["ev"] if ops[d]["inc"] != 1 or ops[d]["q"] is None else ("op", d)
                Q[q].wait_ge(where[w][0], where[w][1])
                for m in (members[w] if w[0] != "op" else [d]):
                    assert m < i
                    know[q] |= at[m]
            if o["fn"] is None:
                at.append(0)
                continue
            ins = o["fn"]()
            if o["inc"] == 1:
                count[q] += 1
                done[q] |= know[q] | (1 << i)
                at.append(done[q])
                where[("op", i)] = (T.sem["c" + q], count[q])
                ins.then_inc(T.sem["c" + q], 1)
            elif o["inc"] == 16:
                at.append(know[q] | (1 << i))
                if ev not in where:
                    where[ev] = (T.sem["e%d" % ndma[0]], 16 * len(members[ev]))
                    ndma[0] += 1
                ins.then_inc(where[ev][0], 16)
            else:
                at.append(know[q])
        for q in "vapg":
            g.wait_ge(T.sem["c" + q], count[q])

    def ts(out, in0, s1, s2, op0, op1=None, grp=None):
        def fn():
            if op1 is None:
                return g.vector.tensor_scalar(ap(out), ap(in0), ap(s1), None, op0)
            return g.vector.tensor_scalar(ap(out), ap(in0), ap(s1), ap(s2), op0, op1)
        return op("v", fn, [in0, s1, s2], [out], grp)

    def tt(out, in0, in1, o, grp=None):
        return op("v", lambda: g.vector.tensor_tensor(ap(out), ap(in0), ap(in1), o), [in0, in1], [out], grp)

    def cp(out, in_, grp=None):
        return op("v", lambda: g.vector.tensor_copy(ap(out), ap(in_)), [in_], [out], grp)

    def scan(out, d0, d1, init, op0, op1, grp=None):
        return op("v", lambda: g.vector.tensor_tensor_scan(ap(out), ap(d0), ap(d1), ap(init), op0, op1), [d0, d1, init], [out], grp)

    def zero(out, grp=None, c=0.0):
        return op("v", lambda: g.vector.memset(ap(out), c), [], [out], grp)

    def trp(out, in_, grp=None):
        return op("v", lambda: g.vector.transpose(ap(out), ap(in_)), [in_], [out], grp)

    def quant(q, s, in_):
        return op("v", lambda: g.vector.quantize_mx(ap(q), ap(s), ap(in_)), [in_], [q, s])

    def act(out, in_, f, bias=None, scale=None, accum=None, grp=None):
        def fn():
            kw = {}
            if bias is not None:
                kw["bias"] = ap(bias)
            if scale is not None:
                kw["scale"] = ap(scale)
            if accum is not None:
                kw["accum_out"] = ap(accum)
            return g.scalar.activation(ap(out), ap(in_), f, **kw)
        return op("a", fn, [in_, bias, scale], [out] + ([accum] if accum is not None else []), grp)

    def fill(out, m, c, grp=None):
        return act(out, V("zs", 0, m), ACT.Identity, bias=c, grp=grp)

    def mm(out, w, ws, x, xs, start=True, stop=True, grp=None):
        return op("p", lambda: g.tensor.matmul_mx(ap(out), ap(w), ap(ws), ap(x), ap(xs), start, stop), [w, ws, x, xs], [out], grp, acc=not start)

    def dma(q, out, in_, reads, writes, grp=None):
        return op(q, lambda: Q[q].dma_start(out, in_), reads, writes, grp, inc=16)

    def iota(out, pattern, base, cm=0, small=True):
        def fn():
            if small:
                return g.iota(ap(out), pattern, base, cm, allow_small_or_imprecise_dtypes=True)
            return g.iota(ap(out), pattern, base, cm)
        return op("g", fn, [], [out])

    def asel(out, in_, pattern, cmp, base, cm, grp=None):
        return op("g", lambda: g.affine_select(ap(out), ap(in_), pattern, cmp, 0.0, base, cm), [in_], [out], grp)

    sent = [0]

    def send(t, which):
        dst = T.cores[(rank - 1) % n] if which == 0 else T.cores[(rank + J) % n]
        src = (rank + 1) % n if which == 0 else (rank - J) % n
        names = ("q%d" % t, "s%d" % t, 0, H, C, E) if which == 0 else ("aq%d" % t, "as%d" % t, K, 2 * K, 0, K)
        sem = T.sem["hf"[which] + str(t)]
        for part in range(2):
            to = rt[rank][0][part] if rt[rank][1][which] else dst
            rid, pid = topo.addr(to, core)
            s_, d_ = pieces(T, t, which)[part]
            sent[0] += len(topo.engines(core, to))
            op("g", lambda s_=s_, d_=d_, rid=rid, pid=pid, to=to: g.remote_dma(d_, s_, sem, T.sem.sent, pid, rid, topo.mask(core, to)),
               [V(names[part], names[2], names[3])], [], inc=0)
        total = 0
        for part in range(2):
            last = rt[src][0][part] if rt[src][1][which] else T.cores[src]
            total += len(topo.engines(last, core))
        op(None, None, [], [V(names[0], names[4], names[5]), V(names[1], names[4], names[5])], fixed=(sem, total))

    RC, R4, B4, PR, GP, GI, YC, OFW, OFV, NV, RG, R33, YG, PR2, NG = [V("cf", i, i + 1) for i in range(15)]

    dma("s", T.x0[:, 0:512], T.x[:, 0:512], [], [V("x0", 0, 512)])
    dma("s", T.ut[:], T.u[:], [], [V("ut")])
    dma("s", T.x0[:, 512:4 * C], T.x[:, 512:4 * C], [], [V("x0", 512, 4 * C)])

    def slot(k, lo, hi):
        if k == 24 and lo >= C:
            k = 2
        c = [k in tile for tile in TILES].index(True)
        e = TILES[c].index(k)
        return V("ta", 4 * (BASE[c] + lo) + e, 4 * (BASE[c] + hi), 4)

    def hole(c):
        zero(V("ta", 4 * (BASE[c] + 16 * min(TILES[c])), 4 * (BASE[c] + WIDE[c])), "hole")

    P = V("ci", 7, 8)
    iota(P, [[0, 1]], 0, 1, False)
    iota(V("t16"), [[0, 24], [1, 16]], 0)
    iota(V("expi"), [[16, 8]], 0, 0, False)
    iota(V("kc", 0, 24), [[16, 24]], 0)
    iota(V("kc", 24, 52), [[-32, 7], [-16, 4]], 17)
    zero(V("zs"))
    ts(V("ci", 0, 1), P, 15, None, A.bitwise_and, grp="ci")
    ts(V("ci", 4, 5), P, 4, 1, A.arith_shift_right, A.bitwise_and, grp="ci")
    ts(V("ci", 1, 2), P, 2, 3, A.arith_shift_right, A.bitwise_and, grp="ci")
    ts(V("ci", 2, 3), P, 3, None, A.bitwise_and, grp="ci")
    ts(V("ci", 5, 6), P, 4, None, A.arith_shift_right, grp="ci")
    tt(V("ci", 6, 7), V("ci", 0, 1), V("ci", 4, 5), A.add)
    cp(RC, V("ci", 0, 1))
    hole(3)
    ts(V("ci", 3, 4), V("ci", 6, 7), 1, None, A.bitwise_and)
    hole(1)
    ts(V("maskw"), V("t16"), RC, None, A.is_equal)
    cp(V("cf", 1, 6), V("ci", 1, 6))
    cp(V("pku"), V("expi"))
    fill(V("bz", 0, E), E, -1024.0)
    fill(V("bz", E, 2 * E), E, -1024.0)
    act(V("rstw"), V("t16"), ACT.Identity, bias=-BIG, scale=2 * BIG)
    act(V("capw"), V("maskw"), ACT.Identity, bias=-BIG, scale=2 * BIG)
    act(OFW, RC, ACT.Identity, bias=7680.0, scale=-512.0, grp="pad0")
    act(R33, RC, ACT.Identity, bias=6400.0 - 7680.0, scale=545.0, grp="pad0")
    act(YG, GP, ACT.Identity, bias=RC, scale=16.0, grp="pad0")
    act(PR2, PR, ACT.Identity, bias=15.0, scale=304.0, grp="pad0")
    act(RG, R4, ACT.Identity, bias=B4, scale=-2048.0, grp="pad0")
    fill(V("jv", JW - 1, JW), 1, 0.0, "pad")
    act(V("ycw", 0, 24), V("kc", 26, 50), ACT.Identity, bias=RC, grp="pad")
    act(V("ygf"), V("kc", 0, 24), ACT.Identity, bias=YG, scale=2.0, grp="pad2")

    def consts_act1():
        act(V("ycw", 18, HALOV + 1), V("ycw", 18, HALOV + 1), ACT.Identity, bias=128.0)
        for k in TILES[5]:
            hi = C if k == 2 else E
            fill(slot(k, 16 * k, hi), hi - 16 * k, 0.0)

    def consts_v1():
        zero(V("ones"), c=1.0)
        for lo in (128, 256):
            quant(V("ca", BASE[3] + lo, BASE[3] + lo + 128), V("sa", BASE[3] + lo, BASE[3] + lo + 128), V("zs"))

    def consts_v2():
        for e in range(4):
            ts(V("gt", e, 512, 4), V("g1"), GI, None, A.is_equal, grp="gt")
        cp(V("ygo"), V("ygf"))
        ts(V("rgi", 0, 2), V("kc", 0, 2), RC, 16.0, A.add, A.mult)
        ts(V("cs", 0, 4), V("t16", 0, 4), R4, 8704.0, A.is_equal, A.mult)
        quant(GQ, GS, V("gt"))
        ts(V("rgo"), V("rgi", 0, 2), PR2, 607.0, A.add, A.min)

    def consts_act2():
        act(V("cs", 4, 8), V("cs", 0, 4), ACT.Identity, bias=-512.0, grp="pad")
        fill(V("c32"), E, 32.0)
        act(V("cmu"), V("maskw"), ACT.Identity, bias=-512.0, scale=33280.0)
        fill(V("c32", 32, E, 64), 6, 64.0)
        act(V("d0w"), V("kc", 54, 78), ACT.Identity, bias=R33, grp="pad2")
        act(NV, RC, ACT.Identity, bias=-0.5, scale=-1.0, grp="pad2")
        act(OFV, RG, ACT.Identity, bias=6144.0, grp="pad2")
        fill(V("gg", 0, 1), 1, 1024.0)
        fill(V("gg", 1, 2), 1, 0.0)

    def consts_act3():
        for s in range(4):
            act(V("cv", s, E, 4), V("zs", 0, E // 4), ACT.Identity, bias=V("cs", 4 + s, 5 + s), grp="cv")

    def consts_g():
        iota(V("g1"), [[1, 8], [0, 16]], 0)
        for b in range(4):
            asel(V("et", 512 * b, 512 * b + 512), V("ones"), [[-4, 128], [-1, 4]], A.is_equal, b, 4)
            if b == 1:
                iota(V("kc", 52, 80), [[2144, 7], [528, 4]], -1056)
        iota(V("d0k"), [[-2144, 7], [-33, 64]], 1056 - 6400)
        iota(V("tt"), [[1, E]], 0)
        iota(V("kr", 0, 16), [[0, 16]], 0)
        iota(V("kr", 400, 416), [[0, 16]], -32768)
        iota(V("smn", E, E + 16), [[0, 16]], 4096)
        iota(V("posc"), [[32, 24]], 15)
        iota(V("cm", 0, 1), [[0, 1]], 1024)
        iota(V("negt"), [[-1, C]], 0)
        iota(V("xp", 0, 16), [[0, 16]], 0)
        iota(V("xp", 304, 320), [[0, 16]], 0)
        iota(V("segr"), [[0, 38], [4096, 16]], -2048)
        iota(V("at", 4 * K, 512), [[0, 4 * K]], 0)
        dma("g", T.vt[:], T.v[:], [], [V("vt")])

    GQ, GS = V("gq"), V("gs")
    FB = ["d0", "d1", "d2", "pb"]

    def sw(k):
        return V("sc", 16 * k + 15, 16 * k + 16)

    fin = []
    for t in range(R):
        X, XN = "x%d" % t, "x%d" % (t + 1)
        q, s = "q%d" % t, "s%d" % t
        aq, as_ = "aq%d" % t, "as%d" % t
        last = t == R - 1
        quant(V(q, 0, 128), V(s, 0, 128), V(X, 0, 512))
        send(t, 0)
        if t == 0:
            dma("s", T.wq[:].bitcast(dt.uint8), T.wc[:], [V(q, C, E)], [V("wq")])
            dma("s", T.wp[:], T.ws[:], [], [V("wp")])
            zero(V("rst32"), c=8192.0)
            quant(V("uq"), V("us"), V("ut"))
            hole(0)
            hole(2)
            hole(4)
            zero(V("rst32", 0, 768, 32), c=-1024.0)
            op("v", lambda: g.vector.tensor_copy(T.urq[:].bitcast(dt.uint32), T.uq[:].bitcast(dt.uint32).indirect(T.pku[:])), [V("uq"), V("pku")], [V("urq")])
            act(V("urs"), ind(V("us"), V("pku")), ACT.Copy)
        quant(V(q, 128, C), V(s, 128, C), V(X, 512, 4 * C))
        if t == 0:
            consts_v1()
            consts_act1()
            consts_g()

        def score(bank, lo, hi):
            mm(V(bank, 0, hi - lo), V("urq"), V("urs"), V(q, lo, hi), V(s, lo, hi))

        def hold(lo, hi):
            scan(V("sc", lo, hi), V("rstw", lo, hi), V("mm", lo, hi), 0.0, A.min, A.max)

        def cmp_v(k, bank="pa"):
            ts(slot(k, 0, min(C, 16 * k)), V(bank, 0, min(C, 16 * k)), sw(k), None, A.is_lt)

        def count_v(k, grp=None):
            scan(V("jv", JW * k + JW - 16 * k, JW * k + JW), slot(k, 0, 16 * k), V("zs", 0, 16 * k), -128.0 if k > 16 else 0.0, A.add, A.add)

        def runs(lo, hi):
            scan(V("rd", lo, hi), V("t16", lo, hi), slot(24, lo, hi), 0.0, A.min, A.add)

        def qa(c, lo, hi):
            quant(V("ca", BASE[c] + lo, BASE[c] + hi), V("sa", BASE[c] + lo, BASE[c] + hi), V("ta", 4 * (BASE[c] + lo), 4 * (BASE[c] + hi)))

        def both(ks, bank, grp):
            for k in ks:
                act(slot(k, 0, 16 * k), V(bank, 0, 16 * k), ACT.Sign, bias=sw(k), scale=-1.0)
            for k in ks:
                act(slot(k, 0, 16 * k), slot(k, 0, 16 * k), ACT.Relu, accum=V("rs", k, k + 1), grp=grp)

        def na(c, first=False, end=False):
            w = ROOM[c]
            mm(V("na", 0, w), GQ, GS, V("ca", BASE[c], BASE[c] + w), V("sa", BASE[c], BASE[c] + w), first, end, grp=("na", t))

        def unpack(b, product=True, copy=True):
            if product:
                mm(V(FB[b], 0, E), V("eq", 128 * b, 128 * b + 128), V("es", 128 * b, 128 * b + 128), V(q, 0, E), V(s, 0, E))
            if copy:
                act(V("ft", b, 4 * E, 4), V(FB[b], 0, E), ACT.Copy)

        def pack_e(b):
            quant(V("eq", 128 * b, 128 * b + 128), V("es", 128 * b, 128 * b + 128), V("et", 512 * b, 512 * b + 512))

        score("pa", 0, C)
        score("pb", 0, C)
        cuts = list(zip(SCUT[1:], SCUT[:-1]))
        for lo, hi in cuts:
            tt(V("mm", lo, hi), V("pa", lo, hi), V("capw", lo, hi), A.min)
        for lo, hi in cuts:
            hold(lo, hi)
        both((17, 16, 15), "pb", ("both", t, 0))
        both(range(14, OWNV, -1), "pb", ("both", t, 1))
        for k in range(OWNV, OWNV - 3, -1):
            cmp_v(k)
        tt(slot(24, 0, C), V("pa", 0, C), V("sc", 0, C), A.is_le)
        for k in range(OWNV - 3, 0, -1):
            cmp_v(k)
        runs(0, C)
        for k in range(OWNV, 0, -1):
            count_v(k)
        tt(V("rdc", 0, 18), V("rd", 15, C, 16), V("ycw", 0, 18), A.add)
        qa(3, 0, WIDE[3])

        def counts(step, lo, hi):
            if step == 0:
                tt(V("bz", 32 * lo, 32 * hi, 32), V("rdc", lo, hi), V("rs", lo, hi), A.add)
            elif step == 5:
                tt(V("bz", 32 * lo, 32 * hi, 32), V("rdc", lo, hi), V("jv", JW * lo + JW - 1, JW * hi, JW), A.add)
            elif step == 1:
                scan(V("bh", 32 * lo, 32 * hi), V("rst32", 32 * lo, 32 * hi), V("bz", 32 * lo, 32 * hi), 0.0, A.min, A.max)
            elif step == 2:
                trp(V("bt", 32 * lo, 32 * hi), V("bh", 32 * lo, 32 * hi))
            elif step == 3:
                ts(V("rr", 16 * lo, 16 * hi), ind(V("bt", 0, 32 * hi), V("ygo", lo, hi)), 6159.5, None, A.add)
            else:
                act(V("rr", 16 * lo, 16 * hi), ind(V("bt", 0, 32 * hi), V("ygo", lo, hi)), ACT.Identity, bias=6159.5)

        steps = [lambda: qa(0, 0, WIDE[0]), lambda: counts(5, 0, OWNV + 1), lambda: counts(0, OWNV + 1, 18), lambda: qa(1, 0, WIDE[1]),
                 lambda: counts(1, 0, 18), lambda: qa(2, 0, WIDE[2]), lambda: counts(2, 0, 18), lambda: counts(4, 0, 18)]
        early = EARLY if t == 0 else 1

        def step(i):
            if i >= early:
                steps[i]()

        for i in range(early):
            steps[i]()
            if i == 1 and t == 0:
                consts_v2()
            if i in (3, 4, 5):
                pack_e(i - 3)
        if t == 0:
            consts_act2()
            consts_act3()
        score("ph", 256, E)
        score("pd", 0, E)
        tt(V("mm", C, E), V("ph", C - 256, 128), V("capw", C, E), A.min)
        step(1)
        na(3, True)
        na(0)
        hold(C, E)
        step(3)
        na(1)
        both(range(23, HALOV, -1), "pd", ("both", t, 2))
        for k in range(HALOV, 18, -1):
            ts(slot(k, C, 16 * k), V("ph", C - 256, 16 * k - 256), sw(k), None, A.is_lt)
        tt(slot(24, C, E), V("ph", C - 256, 128), V("sc", C, E), A.is_le)
        cmp_v(19)
        runs(C, E)
        step(2)
        cmp_v(18)
        step(4)
        for k in range(20, HALOV + 1):
            cmp_v(k)
        step(6)
        step(7)
        for b in range(2 if t == 0 else 4):
            unpack(b, True, b < 2)
        tt(V("rdc", 18, 24), V("rd", C + 15, E, 16), V("ycw", 18, 24), A.add)
        for k in range(18, HALOV + 1):
            count_v(k)
        qa(5, 0, WIDE[5])
        counts(0, HALOV + 1, 24)
        counts(5, 18, HALOV + 1)
        qa(4, 0, WIDE[4])
        counts(1, 18, 24)
        step(5)
        counts(2, 18, 24)
        counts(4, 18, 24)
        if t == 0:
            pack_e(3)

        order = (5, 4, 2) if t > 0 else (2, 5, 4)
        for c in order:
            na(c, False, c == order[-1])
        for b in range(2, 2 + NFL[t > 0]):
            unpack(b, t == 0)
        for lo, hi in ((0, KCUT), (KCUT, E)):
            tt(V("yb", lo, hi), V("rr", lo, hi), V("na", lo, hi), A.subtract)
        for lo, hi in ((0, KCUT), (KCUT, E)):
            scan(V("ext", lo, hi), V("cmu", lo, hi), V("yb", lo, hi), 0.0, A.add, A.min)
            scan(V("kr", 16 + lo, 16 + hi), V("d0k", 32 + lo, 32 + hi), V("yb", lo, hi), 0.0, A.min, A.add)
            if lo == 0:
                scan(V("cmx"), V("c32"), V("yb"), 8192.0, A.add, A.min)
            else:
                scan(V("df"), V("smn", 1, E + 1), V("cmx"), 0.0, A.max, A.subtract)
            tt(V("kw", lo // 16, hi // 16), V("d0w", lo // 16, hi // 16), V("ext", lo + 15, hi, 16), A.subtract)
            if lo == 0:
                scan(V("smn", E - 1, None, -1), V("yb", E - 1, None, -1), V("c32", E - 1, None, -1), 0.0, A.max, A.subtract)
        for k in range(24):
            act(V("junk", 36 * k, 36 * k + 36), V("kr", 6 + 16 * k, 42 + 16 * k), ACT.Sign, bias=V("kw", k, k + 1), accum=V("sg", k, k + 1))
            if k == FLK:
                act(V("fl"), V("df"), ACT.Sign)
            if k == CMK:
                if FLK < 0:
                    ts(V("fl"), V("df"), 0.0, None, A.is_gt)
                act(V("cm", 1, E + 1 if last else C + 1), V("fl", 0, E if last else C), ACT.Identity, scale=-1025.0, bias=1024.0)
        for b in range(2 + NFL[t > 0], 4):
            unpack(b, t == 0)

        def position(step, h):
            lo, hi = PCUT[h], PCUT[h + 1]
            if step == 0:
                tt(V("p2", lo, hi), V("sg", lo, hi), V("posc", lo, hi), A.add)
            elif step == 1:
                ts(V("pso", lo, hi), V("p2", lo, hi), 0.5, None, A.mult)
            else:
                cp(ind(V("orr"), V("pso", lo, hi)), V("tt", 16 * lo, 16 * hi))

        position(0, 0)
        scan(V("bend", E - 1, None, -1), V("fl", E - 1, None, -1), V("tt", E - 1, None, -1), 0.0, A.mult, A.max)
        position(1, 0)

        JC = 16 * PCUT[1] - 16

        def far(step, lo, hi):
            if step == 0:
                scan(V("dd", lo, hi), V("negt", lo, hi), V("orr", lo, hi), 0.0, A.min, A.add)
                act(V("da", lo, hi), V("dd", lo, hi), ACT.Abs)
            elif step == 1:
                act(V("jk2", lo, hi), V("da", lo, hi), ACT.Sign, bias=NV, accum=V("sv") if lo == 0 else V("ii", 0, 1))
            elif step == 2:
                ts(V("ii", lo + 1, hi + 1), V("da", lo, hi), RC, 1026.0, A.is_equal, A.mult)
            elif step == 3:
                ts(V("gg", lo + 2, hi + 2), V("da", lo, hi), RC, 1024.0, A.is_equal, A.mult)
            elif step == 4:
                scan(V("ov", lo, hi), V("cv", lo, hi), V("orr", lo, hi), 0.0, A.add, A.min)
            else:
                ts(V("ovo", lo // 4, hi // 4), V("ov", lo + 3, hi, 4), 4.0, OFV, A.mult, A.add)

        def gather_o(lo, hi):
            act(V(XN, 16 * lo, 16 * hi), ind(V("ft"), V("ovo", lo, hi)), ACT.Copy)

        position(2, 0)
        position(0, 1)
        far(4, 0, JC)
        position(1, 1)
        if SPLIT:
            far(0, 0, JC)
        far(5, 0, JC)
        if SPLIT:
            far(1, 0, JC)
        gather_o(0, FCUT[0])
        scan(V("mu", 0, C), V("cm", 0, C), V("bend", 0, C), 0.0, A.add, A.min)
        position(2, 1)
        position(0, 2)
        lo = JC if SPLIT else 0
        if SPLIT:
            far(2, 0, JC)
        position(1, 2)
        far(0, lo, C)
        if SPLIT:
            far(3, 0, JC)
        JD = 16 * PCUT[2] - 16
        far(4, JC, JD)
        position(2, 2)
        far(5, JC, JD)
        gather_o(FCUT[0], FCUT[1])
        far(1, lo, C)
        gather_o(FCUT[1], JD // 4)
        far(2, lo, C)
        far(3, lo, C)
        far(4, JD, E)
        if SPLIT:
            scan(V("xp", 15, 304), V("ii"), V("gg", 0, C + 1), V("sv"), A.add, A.subtract)
        else:
            scan(V("xp", 16, 304), V("ii", 1, C + 1), V("gg", 1, C + 1), V("sv"), A.add, A.subtract)
        far(5, JD, E)
        if FCUT[2] > JD // 4:
            gather_o(JD // 4, FCUT[2])
        scan(V("mv"), V("cv", 0, C), V("mu", 0, C), 0.0, A.add, A.min)
        trp(V("tr", 0, C), V("xp", 16, 304))
        trp(V("tr", C, 608), V("xp"))
        ts(V("mvo"), V("mv", 3, C, 4), 4.0, OFV, A.mult, A.add)
        scan(V("sgm", 0, C), V("segr", 0, C), V("tr", 0, C), 0.0, A.min, A.max)
        scan(V("sgm", C, 608), V("segr", C, 608), V("tr", C, 608), 0.0, A.min, A.max)
        if FCUT[2] < 96:
            cp(V(XN, 16 * FCUT[2], 4 * E), ind(V("ft"), V("ovo", FCUT[2], 96)))
        act(V("hm", 0, 16 * HCUT[0]), ind(V(XN), V("mvo", 0, HCUT[0])), ACT.Identity, scale=-0.5)
        ts(V("rko"), ind(V("sgm"), V("rgo")), 0.5, 143.0, A.mult, A.add)
        cp(ind(V("er"), V("rko", 0, 18)), V("tt", 0, C))

        def gather_m(h):
            if HCUT[h + 1] > HCUT[h]:
                ts(V("hm", 16 * HCUT[h], 16 * HCUT[h + 1]), ind(V(XN), V("mvo", HCUT[h], HCUT[h + 1])), -0.5, None, A.mult)

        gather_m(0)
        scan(V("ev"), V("cv", 0, K), V("er", 0, K), 0.0, A.add, A.min)
        gather_m(1)
        ts(V("evo"), V("ev", 3, K, 4), 4.0, OFV, A.mult, A.add)
        if last:
            scan(V("mu", C, E), V("cm", C, E), V("bend", C, E), V("mu", C - 1, C), A.add, A.min)
        for h in range(2):
            cp(V("t2", 128 * h, 128 * h + 128), ind(V(XN, 0, 4 * C), V("evo", 8 * h, 8 * h + 8)))
        for h in range(2):
            act(V("t1", 128 * h, 128 * h + 128), ind(V("hm"), V("evo", 8 * h, 8 * h + 8)), ACT.Copy)
            tt(V("at", 128 * h, 128 * h + 128), V("t1", 128 * h, 128 * h + 128), V("t2", 128 * h, 128 * h + 128), A.add)
        quant(V(aq, K, 192), V(as_, K, 192), V("at"))
        send(t, 1)
        op("g", lambda XN=XN: g.dma_start(T[XN][:, ZD:4 * C], T.hm[:, ZD:4 * C], accum_op=A.add), [V("hm", ZD, 4 * C), V(XN, ZD, 4 * C)],
           [V(XN, ZD, 4 * C)], inc=16)
        act(V("a32"), V("at", 0, 4 * K), ACT.Identity, scale=32.0)
        if last:
            scan(V("muw"), V("cmu"), V("mu"), 0.0, A.add, A.min)
        tt(V(XN, 0, ZD), V(XN, 0, ZD), V("hm", 0, ZD), A.add)
        if last:
            ts(V("muo"), V("muw", 15, E, 16), OFW, None, A.add)
            act(V("mr"), ind(V("orr"), V("muo")), ACT.Copy)
            fin.append(dma("a", T.lm[:], T.mr[0:128:16, :], [V("mr")], []))
        else:
            quant(V("vq"), V("vs"), V("vt"))
        for b in range(4):
            mm(V(FB[b], 0, 128), V("wq", 128 * b, 128 * b + 128), V("wp", 128 * b, 128 * b + 128), V(aq, 0, 128), V(as_, 0, 128))
        for b in range(4):
            tt(V("n32", b, 4 * K, 4), V(FB[b], 0, K), V("a32", b, 4 * K, 4), A.add, grp=("n32", t))
        ts(V("nw"), V("n32"), 0.03125, None, A.mult)
        cp(ind(V(XN, 0, 4 * C), V("evo")), V("nw"))

    q, s = "q%d" % R, "s%d" % R
    hc = C // 2
    quant(V(q, 0, hc), V(s, 0, hc), V("x%d" % R, 0, 4 * hc))
    quant(V(q, hc, C), V(s, hc, C), V("x%d" % R, 4 * hc, 4 * C))
    mm(V("pa", 0, hc), V("vq"), V("vs"), V(q, 0, hc), V(s, 0, hc))
    mm(V("pd", 0, hc), V("vq"), V("vs"), V(q, hc, C), V(s, hc, C))
    act(V("yo", 0, hc), V("pa", 0, hc), ACT.Copy)
    cp(V("yo", hc, C), V("pd", 0, hc))
    fin.append(dma("s", T.oc[:], T[q][:, 0:C].bitcast(dt.uint8), [V(q, 0, C)], [], grp="outs"))
    fin.append(dma("a", T.y[:], T.yo[:], [V("yo")], []))
    for k in range(4):
        fin.append(dma("s", T.osc[4 * k:4 * k + 4, :], T[s][32 * k:32 * k + 4, 0:C], [V(s, 0, C)], [], grp="outs"))
    ops.append({"q": "g", "fn": None, "deps": set(fin), "ev": ("end",), "inc": 0, "fixed": None})
    emit()
    g.wait_ge(T.sem.sent, sent[0])
